import numpy as np
import ml_dtypes


def mxq(x, axis, fmt="e4m3"):
    dtype, down = {"e4m3": (ml_dtypes.float8_e4m3fn, 7), "e5m2": (ml_dtypes.float8_e5m2, 14)}[fmt]
    v = np.moveaxis(np.asarray(x, np.float32).astype(ml_dtypes.bfloat16).astype(np.float64), axis, -1)
    blocks = v.reshape(v.shape[:-1] + (-1, 32))
    amax = np.abs(blocks).max(-1, keepdims=True)
    byte = np.maximum(np.where(amax > 0, np.frexp(amax)[1] - 1 + 127, 0) - down, 1)
    scale = np.exp2(byte - 127.0)
    codes = (blocks / scale).astype(np.float32).astype(dtype).astype(np.float64)
    return np.moveaxis((codes * scale).reshape(v.shape), -1, axis)


WIDE = False


def mx_kscale(k):
    if not WIDE:
        return np.ones(k)
    levels = np.array([10, -10, 5, -5, 0])
    if k % 512:
        return np.exp2(np.random.permutation(np.resize(levels, k // 32))).repeat(32)
    a = np.empty((k // 512, 16))
    for p in range(k // 512):
        a[p, :8] = np.random.permutation(np.resize(levels, 8))
        for g in range(8):
            far = levels[np.abs(levels - a[p, g]) >= 10]
            a[p, g + 8] = far[np.random.randint(len(far))]
    return np.exp2(a.ravel()).repeat(32)


def f64(x):
    return np.asarray(x).astype(np.float64)


def striped(idx):
    return np.tile(idx.reshape(-1, 16).T, (8, 1)).astype(np.uint16)


def unstriped(offs):
    return offs[:16].T.reshape(-1).astype(np.int64)


def pack_weight(w):
    k, n = w.shape
    w = f64(np.asarray(w, np.float32).astype(ml_dtypes.bfloat16)).reshape(k // 32, 32, n)
    amax = np.abs(w).max(1)
    byte = np.clip(np.where(amax > 0, np.frexp(amax)[1] - 1 + 127 - 7, 1), 1, 254)
    scaled = (w * np.exp2(127.0 - byte)[:, None, :]).reshape(k, n).astype(np.float32)
    words = np.ascontiguousarray(scaled.reshape(k // 512, 128, 4, n).transpose(0, 1, 3, 2)).astype(ml_dtypes.float8_e4m3fn).view(np.uint8)
    return words, np.ascontiguousarray(byte.astype(np.uint8).reshape(k // 512, 16, n))


def unpack_weight(words, scales):
    g, p, n, _ = words.shape
    vals = np.ascontiguousarray(words).view(ml_dtypes.float8_e4m3fn).astype(np.float64) * np.repeat(np.exp2(scales.astype(np.float64) - 127.0), 8, axis=1)[..., None]
    return vals.transpose(0, 1, 3, 2).reshape(g * 512, n)


K, T, E, C, N = 1024, 512, 8, 128, 128


def by_expert(wq, xq):
    return np.concatenate([wq[e].T @ xq[:, e * C:(e + 1) * C] for e in range(E)], axis=1)


def setup_inputs():
    n = np.random.standard_normal
    s = mx_kscale(K)[:, None]
    first = np.random.permutation(np.repeat(np.arange(E), T // E))
    second = (first + 1 + np.random.permutation(np.repeat(np.arange(E - 1), -(-T // (E - 1)))[:T])) % E
    while np.bincount(second, minlength=E).max() != T // E:
        load = np.bincount(second, minlength=E); hi, lo = int(load.argmax()), int(load.argmin())
        t = np.flatnonzero((second == hi) & (first != lo))[0]; second[t] = lo
    slot_token = np.empty(E * C, np.int64); pos = np.empty((2, T), np.int64); fill = np.zeros(E, np.int64)
    place = np.stack([np.random.permutation(C) for _ in range(E)])
    for r, deal in enumerate((first, second)):
        for t in np.random.permutation(T):
            e = deal[t]; j = e * C + place[e, fill[e]]; fill[e] += 1; slot_token[j] = t; pos[r, t] = j
    g = np.random.uniform(0.2, 0.8, T)
    packed = [pack_weight(m) for m in n((E, K, N)) / np.sqrt(K) / s[None]]
    return {
        "xT": (n((K, T)) * s).astype(np.float32),
        "w_words": np.stack([m[0] for m in packed]),
        "w_scales": np.stack([m[1] for m in packed]),
        "gate": np.stack([np.tile(g, (N, 1)), np.tile(1.0 - g, (N, 1))]).astype(np.float32),
        "offs": striped(slot_token),
        "pos1": striped(pos[0]),
        "pos2": striped(pos[1]),
    }


def reference(xT, w_words, w_scales, gate, offs, pos1, pos2):
    idx = unstriped(offs)
    xq = mxq(f64(xT)[:, idx], 0, "e4m3")
    w = np.stack([unpack_weight(w_words[e], w_scales[e]) for e in range(E)])
    y = by_expert(w, xq)
    return f64(gate[0]) * y[:, unstriped(pos1)] + f64(gate[1]) * y[:, unstriped(pos2)]

@@ -1,0 +1,134 @@
+from contextlib import ExitStack
+
+import concourse.mybir as mybir
+
+K, T, E, C, N = 1024, 512, 8, 128, 128
+SLOTS = E * C
+PASSES = K // 512
+P = 128
+FLOPS = 2 * K * SLOTS * N
+
+F32 = mybir.dt.float32
+BF16 = mybir.dt.bfloat16
+U32 = mybir.dt.uint32
+I32 = mybir.dt.int32
+U16 = mybir.dt.uint16
+U8 = mybir.dt.uint8
+FP8X4 = mybir.dt.float8_e4m3fn_x4
+MULT = mybir.AluOpType.mult
+ADD = mybir.AluOpType.add
+
+WORD_WINDOW = 1024
+BYTE_WINDOW = 1024
+CHUNKS = (((0, 256, 176), (256, 512, 176)), ((0, 256, 0), (256, 512, 0)))
+QUANT_CUTS = ((0, 256, 512), (0, 512))
+BYTE_CUTS = (0, 512, 896, 1024)
+BANK_CUTS = ((0, 256, 512), (512, 768, 896), (896, 1024))
+OUT_CUT = 320
+
+
+def tile_routed_moe_kernel(tc, xT, w_words, w_scales, gate, offs, pos1, pos2, out):
+    nc = tc.nc
+    with ExitStack() as ctx:
+        lists = ctx.enter_context(tc.tile_pool(name="lists", bufs=1))
+        keep = ctx.enter_context(tc.tile_pool(name="keep", bufs=1))
+        psum = ctx.enter_context(tc.psum_pool(name="psum", bufs=1))
+
+        offs_sb = lists.tile([P, SLOTS // 16], U16, name="offs_sb")
+        pos1_sb = lists.tile([P, T // 16], U16, name="pos1_sb")
+        pos2_sb = lists.tile([P, T // 16], U16, name="pos2_sb")
+
+        words_all = []
+        for a in range(PASSES):
+            words = keep.tile([P, WORD_WINDOW], U32, name="words_all%d" % a, align_bytes=64)
+            nc.vector.memset(words[:, T:].bitcast(I32), 0)
+            words_all.append(words)
+        bytes_all = keep.tile([P, BYTE_WINDOW], U8, name="bytes_all", align_bytes=64)
+        nc.gpsimd.memset(bytes_all[:].bitcast(I32), 0)
+        ws = keep.tile([P, E * PASSES, N], U8, name="ws", align_bytes=64)
+        nc.gpsimd.memset(ws[:].rearrange("p b n -> p (b n)").bitcast(I32), 0)
+
+        raw = {}
+        x_view = xT.rearrange("(a p j) t -> a p j t", p=P, j=4)
+        for a in range(PASSES):
+            for lo, hi, v in CHUNKS[a]:
+                chunk = keep.tile([P, 4, hi - lo], F32, name="raw%d_%d" % (a, lo))
+                nc.sync.dma_start(out=chunk[:], in_=x_view[a, :, :, lo:hi])
+                raw[a, lo] = chunk
+            if a == 0:
+                nc.sync.dma_start(out=offs_sb[:], in_=offs)
+        s_view = w_scales.rearrange("e a q n -> q (e a) n")
+        for q in range(4):
+            nc.sync.dma_start(out=ws[32 * q : 32 * q + 4, :, :].bitcast(I32), in_=s_view[4 * q : 4 * q + 4, :, :].bitcast(I32))
+        ww = keep.tile([P, E * PASSES, 4 * N], U8, name="ww", align_bytes=64)
+        w_view = w_words.rearrange("e a p n r -> p (e a) (n r)")
+        half = E * PASSES // 2
+        for h in range(2):
+            nc.sync.dma_start(out=ww[:, h * half : (h + 1) * half, :], in_=w_view[:, h * half : (h + 1) * half, :])
+        nc.sync.dma_start(out=pos1_sb[:], in_=pos1)
+        nc.sync.dma_start(out=pos2_sb[:], in_=pos2)
+        gates = keep.tile([P, 2, T], F32, name="gates")
+        nc.sync.dma_start(out=gates[:], in_=gate.rearrange("s n t -> n s t"))
+
+        words_slot = keep.tile([P, PASSES, SLOTS], U32, name="words_slot", align_bytes=64)
+        bytes_slot = keep.tile([P, SLOTS], U8, name="bytes_slot", align_bytes=64)
+
+        for a in range(PASSES):
+            grouped = keep.tile([P, T, 4], BF16, name="grouped%d" % a, align_bytes=64)
+            for lo, hi, v in CHUNKS[a]:
+                dst = grouped[:, lo:hi, :].rearrange("p (b i) j -> p b j i", i=4)
+                src = raw[a, lo][:].rearrange("p j (b i) -> p b j i", i=4)
+                nc.scalar.copy(out=dst[:, v // 4 :], in_=src[:, v // 4 :])
+                if v > 0:
+                    nc.vector.tensor_copy(out=dst[:, : v // 4], in_=src[:, : v // 4])
+                if hi in QUANT_CUTS[a]:
+                    cut = QUANT_CUTS[a][list(QUANT_CUTS[a]).index(hi) - 1]
+                    nc.vector.quantize_mx(
+                        out=words_all[a][:, cut:hi].bitcast(FP8X4),
+                        scales=bytes_all[4 * a :, cut:hi],
+                        in_=grouped[:, cut:hi, :].rearrange("p t j -> p (t j)"),
+                    )
+            if a == 0:
+                nc.vector.tensor_copy(out=words_slot[:, 0, :768], in_=words_all[0][:].indirect(offs_sb[:, :48]))
+        nc.vector.tensor_copy(out=words_slot[:, 0, 768:], in_=words_all[0][:].indirect(offs_sb[:, 48:]))
+
+        y = keep.tile([P, SLOTS], F32, name="y")
+        for b in range(len(BYTE_CUTS) - 1):
+            lo, hi = BYTE_CUTS[b], BYTE_CUTS[b + 1]
+            if b == 1:
+                nc.vector.tensor_copy(out=words_slot[:, 1, 512:], in_=words_all[1][:].indirect(offs_sb[:, 32:]))
+            nc.vector.tensor_copy(out=bytes_slot[:, lo:hi], in_=bytes_all[:].indirect(offs_sb[:, lo // 16 : hi // 16]))
+            if b == 0:
+                nc.vector.tensor_copy(out=words_slot[:, 1, :512], in_=words_all[1][:].indirect(offs_sb[:, :32]))
+            for g in range(len(BANK_CUTS[b]) - 1):
+                left, right = BANK_CUTS[b][g], BANK_CUTS[b][g + 1]
+                sums = psum.tile([N, right - left], F32, name="sums%d" % left)
+                for e in range(left // C, right // C):
+                    cols = slice(e * C, (e + 1) * C)
+                    for a in range(PASSES):
+                        nc.tensor.matmul_mx(
+                            out=sums[:, e * C - left : (e + 1) * C - left],
+                            lhsT=ww[:, e * PASSES + a, :].bitcast(FP8X4),
+                            lhsT_scale=ws[:, e * PASSES + a, :],
+                            rhs=words_slot[:, a, cols].bitcast(FP8X4),
+                            rhs_scale=bytes_slot[4 * a :, cols],
+                            start=(a == 0),
+                            stop=(a == PASSES - 1),
+                        )
+                if right == SLOTS:
+                    nc.vector.tensor_copy(out=y[:, left:right], in_=sums[:])
+                else:
+                    nc.scalar.copy(out=y[:, left:right], in_=sums[:])
+
+        first = keep.tile([N, T], F32, name="first")
+        nc.vector.tensor_tensor(first[:], y[:].indirect(pos1_sb[:]), gates[:, 0, :], MULT)
+        pieces = ((0, OUT_CUT), (OUT_CUT, T))
+        seconds = []
+        for lo, hi in pieces:
+            second = keep.tile([N, hi - lo], F32, name="second%d" % lo)
+            nc.vector.tensor_tensor(second[:], y[:].indirect(pos2_sb[:, lo // 16 : hi // 16]), gates[:, 1, lo:hi], MULT)
+            seconds.append(second)
+        for (lo, hi), second in zip(pieces, seconds):
+            total = keep.tile([N, hi - lo], F32, name="total%d" % lo)
+            nc.vector.tensor_tensor(total[:], first[:, lo:hi], second[:], ADD)
+            nc.sync.dma_start(out=out[:, lo:hi], in_=total[:])

@@ -18,13 +18,14 @@ FP8X4 = mybir.dt.float8_e4m3fn_x4
 MULT = mybir.AluOpType.mult
 ADD = mybir.AluOpType.add
 
-WORD_WINDOW = 1024
-BYTE_WINDOW = 1024
-CHUNKS = (((0, 256, 176), (256, 512, 176)), ((0, 256, 0), (256, 512, 0)))
-QUANT_CUTS = ((0, 256, 512), (0, 512))
-BYTE_CUTS = (0, 512, 896, 1024)
-BANK_CUTS = ((0, 256, 512), (512, 768, 896), (896, 1024))
-OUT_CUT = 320
+WORD_WINDOWS = (1408, 704)
+BYTE_WINDOW = 1408
+CHUNKS = (((0, 256, 192), (256, 384, 64), (384, 512, 96)), ((0, 128, 0), (128, 256, 0), (256, 384, 0), (384, 512, 0)))
+QUANT_CUTS = ((0, 256, 384, 512), (0, 256, 512))
+WORD0_CUTS = (0, 1024)
+BYTE_CUTS = (0, 1024)
+WORD1_CUTS = (0, 512, 896, 1024)
+OUT_CUTS = (0, 256, 384, 512)
 
 
 def tile_routed_moe_kernel(tc, xT, w_words, w_scales, gate, offs, pos1, pos2, out):
@@ -40,7 +41,7 @@ def tile_routed_moe_kernel(tc, xT, w_words, w_scales, gate, offs, pos1, pos2, ou
 
         words_all = []
         for a in range(PASSES):
-            words = keep.tile([P, WORD_WINDOW], U32, name="words_all%d" % a, align_bytes=64)
+            words = keep.tile([P, WORD_WINDOWS[a]], U32, name="words_all%d" % a, align_bytes=64)
             nc.vector.memset(words[:, T:].bitcast(I32), 0)
             words_all.append(words)
         bytes_all = keep.tile([P, BYTE_WINDOW], U8, name="bytes_all", align_bytes=64)
@@ -60,11 +61,10 @@ def tile_routed_moe_kernel(tc, xT, w_words, w_scales, gate, offs, pos1, pos2, ou
         s_view = w_scales.rearrange("e a q n -> q (e a) n")
         for q in range(4):
             nc.sync.dma_start(out=ws[32 * q : 32 * q + 4, :, :].bitcast(I32), in_=s_view[4 * q : 4 * q + 4, :, :].bitcast(I32))
-        ww = keep.tile([P, E * PASSES, 4 * N], U8, name="ww", align_bytes=64)
-        w_view = w_words.rearrange("e a p n r -> p (e a) (n r)")
-        half = E * PASSES // 2
-        for h in range(2):
-            nc.sync.dma_start(out=ww[:, h * half : (h + 1) * half, :], in_=w_view[:, h * half : (h + 1) * half, :])
+        ww = keep.tile([P, PASSES, E, 4 * N], U8, name="ww", align_bytes=64)
+        w_view = w_words.rearrange("e a p n r -> a p e (n r)")
+        for a in range(PASSES):
+            nc.sync.dma_start(out=ww[:, a, :, :], in_=w_view[a])
         nc.sync.dma_start(out=pos1_sb[:], in_=pos1)
         nc.sync.dma_start(out=pos2_sb[:], in_=pos2)
         gates = keep.tile([P, 2, T], F32, name="gates")
@@ -73,12 +73,16 @@ def tile_routed_moe_kernel(tc, xT, w_words, w_scales, gate, offs, pos1, pos2, ou
         words_slot = keep.tile([P, PASSES, SLOTS], U32, name="words_slot", align_bytes=64)
         bytes_slot = keep.tile([P, SLOTS], U8, name="bytes_slot", align_bytes=64)
 
+        def gather(dst, window, idx, lo, hi):
+            nc.vector.tensor_copy(out=dst[:, lo:hi], in_=window[:, : max(T, (hi - lo) * 11 // 8)].indirect(idx[:, lo // 16 : hi // 16]))
+
         for a in range(PASSES):
             grouped = keep.tile([P, T, 4], BF16, name="grouped%d" % a, align_bytes=64)
             for lo, hi, v in CHUNKS[a]:
                 dst = grouped[:, lo:hi, :].rearrange("p (b i) j -> p b j i", i=4)
                 src = raw[a, lo][:].rearrange("p j (b i) -> p b j i", i=4)
-                nc.scalar.copy(out=dst[:, v // 4 :], in_=src[:, v // 4 :])
+                if v < hi - lo:
+                    nc.scalar.copy(out=dst[:, v // 4 :], in_=src[:, v // 4 :])
                 if v > 0:
                     nc.vector.tensor_copy(out=dst[:, : v // 4], in_=src[:, : v // 4])
                 if hi in QUANT_CUTS[a]:
@@ -89,46 +93,51 @@ def tile_routed_moe_kernel(tc, xT, w_words, w_scales, gate, offs, pos1, pos2, ou
                         in_=grouped[:, cut:hi, :].rearrange("p t j -> p (t j)"),
                     )
             if a == 0:
-                nc.vector.tensor_copy(out=words_slot[:, 0, :768], in_=words_all[0][:].indirect(offs_sb[:, :48]))
-        nc.vector.tensor_copy(out=words_slot[:, 0, 768:], in_=words_all[0][:].indirect(offs_sb[:, 48:]))
+                for lo, hi in zip(WORD0_CUTS, WORD0_CUTS[1:]):
+                    gather(words_slot[:, 0, :], words_all[0], offs_sb, lo, hi)
 
+        sums = [psum.tile([N, C], F32, name="sums%d" % e) for e in range(E)]
+
+        def multiply(e, a):
+            cols = slice(e * C, (e + 1) * C)
+            nc.tensor.matmul_mx(
+                out=sums[e][:],
+                lhsT=ww[:, a, e, :].bitcast(FP8X4),
+                lhsT_scale=ws[:, e * PASSES + a, :],
+                rhs=words_slot[:, a, cols].bitcast(FP8X4),
+                rhs_scale=bytes_slot[4 * a :, cols],
+                start=(a == 0),
+                stop=(a == PASSES - 1),
+            )
+
+        for lo, hi in zip(BYTE_CUTS, BYTE_CUTS[1:]):
+            gather(bytes_slot, bytes_all, offs_sb, lo, hi)
+            for e in range(lo // C, hi // C):
+                multiply(e, 0)
         y = keep.tile([P, SLOTS], F32, name="y")
-        for b in range(len(BYTE_CUTS) - 1):
-            lo, hi = BYTE_CUTS[b], BYTE_CUTS[b + 1]
-            if b == 1:
-                nc.vector.tensor_copy(out=words_slot[:, 1, 512:], in_=words_all[1][:].indirect(offs_sb[:, 32:]))
-            nc.vector.tensor_copy(out=bytes_slot[:, lo:hi], in_=bytes_all[:].indirect(offs_sb[:, lo // 16 : hi // 16]))
-            if b == 0:
-                nc.vector.tensor_copy(out=words_slot[:, 1, :512], in_=words_all[1][:].indirect(offs_sb[:, :32]))
-            for g in range(len(BANK_CUTS[b]) - 1):
-                left, right = BANK_CUTS[b][g], BANK_CUTS[b][g + 1]
-                sums = psum.tile([N, right - left], F32, name="sums%d" % left)
-                for e in range(left // C, right // C):
-                    cols = slice(e * C, (e + 1) * C)
-                    for a in range(PASSES):
-                        nc.tensor.matmul_mx(
-                            out=sums[:, e * C - left : (e + 1) * C - left],
-                            lhsT=ww[:, e * PASSES + a, :].bitcast(FP8X4),
-                            lhsT_scale=ws[:, e * PASSES + a, :],
-                            rhs=words_slot[:, a, cols].bitcast(FP8X4),
-                            rhs_scale=bytes_slot[4 * a :, cols],
-                            start=(a == 0),
-                            stop=(a == PASSES - 1),
-                        )
-                if right == SLOTS:
-                    nc.vector.tensor_copy(out=y[:, left:right], in_=sums[:])
+        for lo, hi in zip(WORD1_CUTS, WORD1_CUTS[1:]):
+            gather(words_slot[:, 1, :], words_all[1], offs_sb, lo, hi)
+            for e in range(lo // C, hi // C):
+                multiply(e, 1)
+                if e == E - 1:
+                    nc.vector.tensor_copy(out=y[:, e * C : (e + 1) * C], in_=sums[e][:])
                 else:
-                    nc.scalar.copy(out=y[:, left:right], in_=sums[:])
+                    nc.scalar.copy(out=y[:, e * C : (e + 1) * C], in_=sums[e][:])
 
         first = keep.tile([N, T], F32, name="first")
         nc.vector.tensor_tensor(first[:], y[:].indirect(pos1_sb[:]), gates[:, 0, :], MULT)
-        pieces = ((0, OUT_CUT), (OUT_CUT, T))
-        seconds = []
-        for lo, hi in pieces:
+        pieces = list(zip(OUT_CUTS, OUT_CUTS[1:]))
+        seconds = {}
+
+        def finish(lo, hi):
+            total = keep.tile([N, hi - lo], F32, name="total%d" % lo)
+            nc.vector.tensor_tensor(total[:], first[:, lo:hi], seconds[lo][:], ADD)
+            nc.sync.dma_start(out=out[:, lo:hi], in_=total[:])
+
+        for i, (lo, hi) in enumerate(pieces):
             second = keep.tile([N, hi - lo], F32, name="second%d" % lo)
             nc.vector.tensor_tensor(second[:], y[:].indirect(pos2_sb[:, lo // 16 : hi // 16]), gates[:, 1, lo:hi], MULT)
-            seconds.append(second)
-        for (lo, hi), second in zip(pieces, seconds):
-            total = keep.tile([N, hi - lo], F32, name="total%d" % lo)
-            nc.vector.tensor_tensor(total[:], first[:, lo:hi], second[:], ADD)
-            nc.sync.dma_start(out=out[:, lo:hi], in_=total[:])
+            seconds[lo] = second
+            if i > 0:
+                finish(*pieces[i - 1])
+        finish(*pieces[-1])

@@ -20,9 +20,7 @@ ADD = mybir.AluOpType.add
 
 WORD_WINDOWS = (1408, 704)
 BYTE_WINDOW = 1408
-CHUNKS = (((0, 256, 192), (256, 384, 64), (384, 512, 96)), ((0, 128, 0), (128, 256, 0), (256, 384, 0), (384, 512, 0)))
-QUANT_CUTS = ((0, 256, 384, 512), (0, 256, 512))
-WORD0_CUTS = (0, 1024)
+LOAD = 256
 BYTE_CUTS = (0, 1024)
 WORD1_CUTS = (0, 512, 896, 1024)
 OUT_CUTS = (0, 256, 384, 512)
@@ -52,7 +50,8 @@ def tile_routed_moe_kernel(tc, xT, w_words, w_scales, gate, offs, pos1, pos2, ou
         raw = {}
         x_view = xT.rearrange("(a p j) t -> a p j t", p=P, j=4)
         for a in range(PASSES):
-            for lo, hi, v in CHUNKS[a]:
+            for lo in range(0, T, LOAD):
+                hi = lo + LOAD
                 chunk = keep.tile([P, 4, hi - lo], F32, name="raw%d_%d" % (a, lo))
                 nc.sync.dma_start(out=chunk[:], in_=x_view[a, :, :, lo:hi])
                 raw[a, lo] = chunk
@@ -63,12 +62,14 @@ def tile_routed_moe_kernel(tc, xT, w_words, w_scales, gate, offs, pos1, pos2, ou
             nc.sync.dma_start(out=ws[32 * q : 32 * q + 4, :, :].bitcast(I32), in_=s_view[4 * q : 4 * q + 4, :, :].bitcast(I32))
         ww = keep.tile([P, PASSES, E, 4 * N], U8, name="ww", align_bytes=64)
         w_view = w_words.rearrange("e a p n r -> a p e (n r)")
-        for a in range(PASSES):
-            nc.sync.dma_start(out=ww[:, a, :, :], in_=w_view[a])
-        nc.sync.dma_start(out=pos1_sb[:], in_=pos1)
-        nc.sync.dma_start(out=pos2_sb[:], in_=pos2)
+        nc.sync.dma_start(out=ww[:, 0, :, :], in_=w_view[0])
+        nc.sync.dma_start(out=ww[:, 1, : E // 2, :], in_=w_view[1, :, : E // 2, :])
+        nc.sync.dma_start(out=ww[:, 1, E // 2 :, :], in_=w_view[1, :, E // 2 :, :])
         gates = keep.tile([P, 2, T], F32, name="gates")
-        nc.sync.dma_start(out=gates[:], in_=gate.rearrange("s n t -> n s t"))
+        nc.sync.dma_start(out=pos1_sb[:], in_=pos1)
+        nc.sync.dma_start(out=gates[:, 0, :], in_=gate[0])
+        nc.sync.dma_start(out=pos2_sb[:], in_=pos2)
+        nc.sync.dma_start(out=gates[:, 1, :], in_=gate[1])
 
         words_slot = keep.tile([P, PASSES, SLOTS], U32, name="words_slot", align_bytes=64)
         bytes_slot = keep.tile([P, SLOTS], U8, name="bytes_slot", align_bytes=64)
@@ -76,25 +77,32 @@ def tile_routed_moe_kernel(tc, xT, w_words, w_scales, gate, offs, pos1, pos2, ou
         def gather(dst, window, idx, lo, hi):
             nc.vector.tensor_copy(out=dst[:, lo:hi], in_=window[:, : max(T, (hi - lo) * 11 // 8)].indirect(idx[:, lo // 16 : hi // 16]))
 
-        for a in range(PASSES):
-            grouped = keep.tile([P, T, 4], BF16, name="grouped%d" % a, align_bytes=64)
-            for lo, hi, v in CHUNKS[a]:
-                dst = grouped[:, lo:hi, :].rearrange("p (b i) j -> p b j i", i=4)
-                src = raw[a, lo][:].rearrange("p j (b i) -> p b j i", i=4)
-                if v < hi - lo:
-                    nc.scalar.copy(out=dst[:, v // 4 :], in_=src[:, v // 4 :])
-                if v > 0:
-                    nc.vector.tensor_copy(out=dst[:, : v // 4], in_=src[:, : v // 4])
-                if hi in QUANT_CUTS[a]:
-                    cut = QUANT_CUTS[a][list(QUANT_CUTS[a]).index(hi) - 1]
-                    nc.vector.quantize_mx(
-                        out=words_all[a][:, cut:hi].bitcast(FP8X4),
-                        scales=bytes_all[4 * a :, cut:hi],
-                        in_=grouped[:, cut:hi, :].rearrange("p t j -> p (t j)"),
-                    )
-            if a == 0:
-                for lo, hi in zip(WORD0_CUTS, WORD0_CUTS[1:]):
-                    gather(words_slot[:, 0, :], words_all[0], offs_sb, lo, hi)
+        grouped = [keep.tile([P, T, 4], BF16, name="grouped%d" % a, align_bytes=64) for a in range(PASSES)]
+
+        def interleave(copy, a, lo, hi):
+            start = lo // LOAD * LOAD
+            dst = grouped[a][:, lo:hi, :].rearrange("p (b i) j -> p b j i", i=4)
+            src = raw[a, start][:, :, lo - start : hi - start].rearrange("p j (b i) -> p b j i", i=4)
+            copy(out=dst, in_=src)
+
+        def quantise(a, lo, hi):
+            nc.vector.quantize_mx(
+                out=words_all[a][:, lo:hi].bitcast(FP8X4),
+                scales=bytes_all[4 * a :, lo:hi],
+                in_=grouped[a][:, lo:hi, :].rearrange("p t j -> p (t j)"),
+            )
+
+        interleave(nc.scalar.copy, 0, 176, 256)
+        interleave(nc.vector.tensor_copy, 0, 0, 176)
+        quantise(0, 0, 256)
+        interleave(nc.scalar.copy, 0, 432, 512)
+        interleave(nc.vector.tensor_copy, 0, 256, 432)
+        quantise(0, 256, 512)
+        gather(words_slot[:, 0, :], words_all[0], offs_sb, 0, 1024)
+        interleave(nc.scalar.copy, 1, 0, 256)
+        quantise(1, 0, 256)
+        interleave(nc.scalar.copy, 1, 256, 512)
+        quantise(1, 256, 512)
 
         sums = [psum.tile([N, C], F32, name="sums%d" % e) for e in range(E)]
 

@@ -19,11 +19,10 @@ MULT = mybir.AluOpType.mult
 ADD = mybir.AluOpType.add
 
 WORD_WINDOWS = (1408, 704)
-BYTE_WINDOW = 1408
+BYTE_WINDOW = 704
 LOAD = 256
-BYTE_CUTS = (0, 1024)
-WORD1_CUTS = (0, 512, 896, 1024)
-OUT_CUTS = (0, 256, 384, 512)
+WORD1_CUTS = (512, 896, 1024)
+OUT_CUTS = (0, 256, 512)
 
 
 def tile_routed_moe_kernel(tc, xT, w_words, w_scales, gate, offs, pos1, pos2, out):
@@ -60,16 +59,15 @@ def tile_routed_moe_kernel(tc, xT, w_words, w_scales, gate, offs, pos1, pos2, ou
         s_view = w_scales.rearrange("e a q n -> q (e a) n")
         for q in range(4):
             nc.sync.dma_start(out=ws[32 * q : 32 * q + 4, :, :].bitcast(I32), in_=s_view[4 * q : 4 * q + 4, :, :].bitcast(I32))
-        ww = keep.tile([P, PASSES, E, 4 * N], U8, name="ww", align_bytes=64)
-        w_view = w_words.rearrange("e a p n r -> a p e (n r)")
-        nc.sync.dma_start(out=ww[:, 0, :, :], in_=w_view[0])
-        nc.sync.dma_start(out=ww[:, 1, : E // 2, :], in_=w_view[1, :, : E // 2, :])
-        nc.sync.dma_start(out=ww[:, 1, E // 2 :, :], in_=w_view[1, :, E // 2 :, :])
-        gates = keep.tile([P, 2, T], F32, name="gates")
+        ww = keep.tile([P, E * PASSES, 4 * N], U8, name="ww", align_bytes=64)
+        w_view = w_words.rearrange("e a p n r -> p (e a) (n r)")
+        half = E * PASSES // 2
+        for h in range(2):
+            nc.sync.dma_start(out=ww[:, h * half : (h + 1) * half, :], in_=w_view[:, h * half : (h + 1) * half, :])
         nc.sync.dma_start(out=pos1_sb[:], in_=pos1)
-        nc.sync.dma_start(out=gates[:, 0, :], in_=gate[0])
         nc.sync.dma_start(out=pos2_sb[:], in_=pos2)
-        nc.sync.dma_start(out=gates[:, 1, :], in_=gate[1])
+        gates = keep.tile([P, 2, T], F32, name="gates")
+        nc.sync.dma_start(out=gates[:], in_=gate.rearrange("s n t -> n s t"))
 
         words_slot = keep.tile([P, PASSES, SLOTS], U32, name="words_slot", align_bytes=64)
         bytes_slot = keep.tile([P, SLOTS], U8, name="bytes_slot", align_bytes=64)
@@ -104,13 +102,13 @@ def tile_routed_moe_kernel(tc, xT, w_words, w_scales, gate, offs, pos1, pos2, ou
         interleave(nc.scalar.copy, 1, 256, 512)
         quantise(1, 256, 512)
 
-        sums = [psum.tile([N, C], F32, name="sums%d" % e) for e in range(E)]
+        y = keep.tile([P, SLOTS], F32, name="y")
 
-        def multiply(e, a):
+        def multiply(bank, e, a):
             cols = slice(e * C, (e + 1) * C)
             nc.tensor.matmul_mx(
-                out=sums[e][:],
-                lhsT=ww[:, a, e, :].bitcast(FP8X4),
+                out=bank,
+                lhsT=ww[:, e * PASSES + a, :].bitcast(FP8X4),
                 lhsT_scale=ws[:, e * PASSES + a, :],
                 rhs=words_slot[:, a, cols].bitcast(FP8X4),
                 rhs_scale=bytes_slot[4 * a :, cols],
@@ -118,19 +116,26 @@ def tile_routed_moe_kernel(tc, xT, w_words, w_scales, gate, offs, pos1, pos2, ou
                 stop=(a == PASSES - 1),
             )
 
-        for lo, hi in zip(BYTE_CUTS, BYTE_CUTS[1:]):
-            gather(bytes_slot, bytes_all, offs_sb, lo, hi)
-            for e in range(lo // C, hi // C):
-                multiply(e, 0)
-        y = keep.tile([P, SLOTS], F32, name="y")
+        gather(bytes_slot, bytes_all, offs_sb, 0, SLOTS // 2)
+        gather(words_slot[:, 1, :], words_all[1], offs_sb, 0, SLOTS // 2)
+        for pair in range(2):
+            bank = psum.tile([N, 2 * C], F32, name="pair%d" % pair)
+            for i in range(2):
+                for a in range(PASSES):
+                    multiply(bank[:, i * C : (i + 1) * C], 2 * pair + i, a)
+            nc.scalar.copy(out=y[:, 2 * pair * C : 2 * (pair + 1) * C], in_=bank[:])
+
+        gather(bytes_slot, bytes_all, offs_sb, SLOTS // 2, SLOTS)
+        sums = {e: psum.tile([N, C], F32, name="sums%d" % e) for e in range(E // 2, E)}
+        for e in sums:
+            multiply(sums[e][:], e, 0)
         for lo, hi in zip(WORD1_CUTS, WORD1_CUTS[1:]):
             gather(words_slot[:, 1, :], words_all[1], offs_sb, lo, hi)
             for e in range(lo // C, hi // C):
-                multiply(e, 1)
-                if e == E - 1:
-                    nc.vector.tensor_copy(out=y[:, e * C : (e + 1) * C], in_=sums[e][:])
-                else:
-                    nc.scalar.copy(out=y[:, e * C : (e + 1) * C], in_=sums[e][:])
+                multiply(sums[e][:], e, 1)
+        for e in sums:
+            copy = nc.vector.tensor_copy if e >= E - 2 else nc.scalar.copy
+            copy(out=y[:, e * C : (e + 1) * C], in_=sums[e][:])
 
         first = keep.tile([N, T], F32, name="first")
         nc.vector.tensor_tensor(first[:], y[:].indirect(pos1_sb[:]), gates[:, 0, :], MULT)
@@ -142,10 +147,9 @@ def tile_routed_moe_kernel(tc, xT, w_words, w_scales, gate, offs, pos1, pos2, ou
             nc.vector.tensor_tensor(total[:], first[:, lo:hi], seconds[lo][:], ADD)
             nc.sync.dma_start(out=out[:, lo:hi], in_=total[:])
 
-        for i, (lo, hi) in enumerate(pieces):
+        for lo, hi in pieces:
             second = keep.tile([N, hi - lo], F32, name="second%d" % lo)
             nc.vector.tensor_tensor(second[:], y[:].indirect(pos2_sb[:, lo // 16 : hi // 16]), gates[:, 1, lo:hi], MULT)
             seconds[lo] = second
-            if i > 0:
-                finish(*pieces[i - 1])
-        finish(*pieces[-1])
+        for lo, hi in pieces:
+            finish(lo, hi)

@@ -98,8 +98,9 @@ def tile_routed_moe_kernel(tc, xT, w_words, w_scales, gate, offs, pos1, pos2, ou
         quantise(0, 256, 512)
         gather(words_slot[:, 0, :], words_all[0], offs_sb, 0, 1024)
         interleave(nc.scalar.copy, 1, 0, 256)
+        interleave(nc.scalar.copy, 1, 320, 512)
+        interleave(nc.vector.tensor_copy, 1, 256, 320)
         quantise(1, 0, 256)
-        interleave(nc.scalar.copy, 1, 256, 512)
         quantise(1, 256, 512)
 
         y = keep.tile([P, SLOTS], F32, name="y")

@@ -18,10 +18,10 @@ FP8X4 = mybir.dt.float8_e4m3fn_x4
 MULT = mybir.AluOpType.mult
 ADD = mybir.AluOpType.add
 
-WORD_WINDOWS = (1408, 704)
-BYTE_WINDOW = 704
+WORD_WINDOWS = (1408, 880)
+BYTE_WINDOW = 1408
 LOAD = 256
-WORD1_CUTS = (512, 896, 1024)
+WORD1_CUTS = (0, 640, 896, 1024)
 OUT_CUTS = (0, 256, 512)
 
 
@@ -59,11 +59,10 @@ def tile_routed_moe_kernel(tc, xT, w_words, w_scales, gate, offs, pos1, pos2, ou
         s_view = w_scales.rearrange("e a q n -> q (e a) n")
         for q in range(4):
             nc.sync.dma_start(out=ws[32 * q : 32 * q + 4, :, :].bitcast(I32), in_=s_view[4 * q : 4 * q + 4, :, :].bitcast(I32))
-        ww = keep.tile([P, E * PASSES, 4 * N], U8, name="ww", align_bytes=64)
-        w_view = w_words.rearrange("e a p n r -> p (e a) (n r)")
-        half = E * PASSES // 2
-        for h in range(2):
-            nc.sync.dma_start(out=ww[:, h * half : (h + 1) * half, :], in_=w_view[:, h * half : (h + 1) * half, :])
+        ww = keep.tile([P, PASSES, E, 4 * N], U8, name="ww", align_bytes=64)
+        w_view = w_words.rearrange("e a p n r -> a p e (n r)")
+        for a in range(PASSES):
+            nc.sync.dma_start(out=ww[:, a, :, :], in_=w_view[a])
         nc.sync.dma_start(out=pos1_sb[:], in_=pos1)
         nc.sync.dma_start(out=pos2_sb[:], in_=pos2)
         gates = keep.tile([P, 2, T], F32, name="gates")
@@ -98,8 +97,8 @@ def tile_routed_moe_kernel(tc, xT, w_words, w_scales, gate, offs, pos1, pos2, ou
         quantise(0, 256, 512)
         gather(words_slot[:, 0, :], words_all[0], offs_sb, 0, 1024)
         interleave(nc.scalar.copy, 1, 0, 256)
-        interleave(nc.scalar.copy, 1, 320, 512)
-        interleave(nc.vector.tensor_copy, 1, 256, 320)
+        interleave(nc.scalar.copy, 1, 288, 512)
+        interleave(nc.vector.tensor_copy, 1, 256, 288)
         quantise(1, 0, 256)
         quantise(1, 256, 512)
 
@@ -109,7 +108,7 @@ def tile_routed_moe_kernel(tc, xT, w_words, w_scales, gate, offs, pos1, pos2, ou
             cols = slice(e * C, (e + 1) * C)
             nc.tensor.matmul_mx(
                 out=bank,
-                lhsT=ww[:, e * PASSES + a, :].bitcast(FP8X4),
+                lhsT=ww[:, a, e, :].bitcast(FP8X4),
                 lhsT_scale=ws[:, e * PASSES + a, :],
                 rhs=words_slot[:, a, cols].bitcast(FP8X4),
                 rhs_scale=bytes_slot[4 * a :, cols],
@@ -117,24 +116,15 @@ def tile_routed_moe_kernel(tc, xT, w_words, w_scales, gate, offs, pos1, pos2, ou
                 stop=(a == PASSES - 1),
             )
 
-        gather(bytes_slot, bytes_all, offs_sb, 0, SLOTS // 2)
-        gather(words_slot[:, 1, :], words_all[1], offs_sb, 0, SLOTS // 2)
-        for pair in range(2):
-            bank = psum.tile([N, 2 * C], F32, name="pair%d" % pair)
-            for i in range(2):
-                for a in range(PASSES):
-                    multiply(bank[:, i * C : (i + 1) * C], 2 * pair + i, a)
-            nc.scalar.copy(out=y[:, 2 * pair * C : 2 * (pair + 1) * C], in_=bank[:])
-
-        gather(bytes_slot, bytes_all, offs_sb, SLOTS // 2, SLOTS)
-        sums = {e: psum.tile([N, C], F32, name="sums%d" % e) for e in range(E // 2, E)}
-        for e in sums:
+        gather(bytes_slot, bytes_all, offs_sb, 0, SLOTS)
+        sums = [psum.tile([N, C], F32, name="sums%d" % e) for e in range(E)]
+        for e in range(E):
             multiply(sums[e][:], e, 0)
         for lo, hi in zip(WORD1_CUTS, WORD1_CUTS[1:]):
             gather(words_slot[:, 1, :], words_all[1], offs_sb, lo, hi)
             for e in range(lo // C, hi // C):
                 multiply(sums[e][:], e, 1)
-        for e in sums:
+        for e in range(E):
             copy = nc.vector.tensor_copy if e >= E - 2 else nc.scalar.copy
             copy(out=y[:, e * C : (e + 1) * C], in_=sums[e][:])
 

@@ -116,7 +116,8 @@ def tile_routed_moe_kernel(tc, xT, w_words, w_scales, gate, offs, pos1, pos2, ou
                 stop=(a == PASSES - 1),
             )
 
-        gather(bytes_slot, bytes_all, offs_sb, 0, SLOTS)
+        gather(bytes_slot, bytes_all, offs_sb, 0, 3 * SLOTS // 4)
+        gather(bytes_slot, bytes_all, offs_sb, 3 * SLOTS // 4, SLOTS)
         sums = [psum.tile([N, C], F32, name="sums%d" % e) for e in range(E)]
         for e in range(E):
             multiply(sums[e][:], e, 0)
@@ -125,7 +126,7 @@ def tile_routed_moe_kernel(tc, xT, w_words, w_scales, gate, offs, pos1, pos2, ou
             for e in range(lo // C, hi // C):
                 multiply(sums[e][:], e, 1)
         for e in range(E):
-            copy = nc.vector.tensor_copy if e >= E - 2 else nc.scalar.copy
+            copy = nc.vector.tensor_copy if e in (E - 3, E - 2) else nc.scalar.copy
             copy(out=y[:, e * C : (e + 1) * C], in_=sums[e][:])
 
         first = keep.tile([N, T], F32, name="first")

@@ -38,12 +38,12 @@ def tile_routed_moe_kernel(tc, xT, w_words, w_scales, gate, offs, pos1, pos2, ou
 
         words_all = []
         for a in range(PASSES):
-            words = keep.tile([P, WORD_WINDOWS[a]], U32, name="words_all%d" % a, align_bytes=64)
+            words = keep.tile([P, WORD_WINDOWS[a]], U32, name="words_all%d" % a, align_bytes=256)
             nc.vector.memset(words[:, T:].bitcast(I32), 0)
             words_all.append(words)
-        bytes_all = keep.tile([P, BYTE_WINDOW], U8, name="bytes_all", align_bytes=64)
+        bytes_all = keep.tile([P, BYTE_WINDOW], U8, name="bytes_all", align_bytes=256)
         nc.gpsimd.memset(bytes_all[:].bitcast(I32), 0)
-        ws = keep.tile([P, E * PASSES, N], U8, name="ws", align_bytes=64)
+        ws = keep.tile([P, E * PASSES, N], U8, name="ws", align_bytes=256)
         nc.gpsimd.memset(ws[:].rearrange("p b n -> p (b n)").bitcast(I32), 0)
 
         raw = {}
@@ -51,7 +51,7 @@ def tile_routed_moe_kernel(tc, xT, w_words, w_scales, gate, offs, pos1, pos2, ou
         for a in range(PASSES):
             for lo in range(0, T, LOAD):
                 hi = lo + LOAD
-                chunk = keep.tile([P, 4, hi - lo], F32, name="raw%d_%d" % (a, lo))
+                chunk = keep.tile([P, 4, hi - lo], F32, name="raw%d_%d" % (a, lo), align_bytes=256)
                 nc.sync.dma_start(out=chunk[:], in_=x_view[a, :, :, lo:hi])
                 raw[a, lo] = chunk
             if a == 0:
@@ -59,22 +59,22 @@ def tile_routed_moe_kernel(tc, xT, w_words, w_scales, gate, offs, pos1, pos2, ou
         s_view = w_scales.rearrange("e a q n -> q (e a) n")
         for q in range(4):
             nc.sync.dma_start(out=ws[32 * q : 32 * q + 4, :, :].bitcast(I32), in_=s_view[4 * q : 4 * q + 4, :, :].bitcast(I32))
-        ww = keep.tile([P, PASSES, E, 4 * N], U8, name="ww", align_bytes=64)
+        ww = keep.tile([P, PASSES, E, 4 * N], U8, name="ww", align_bytes=256)
         w_view = w_words.rearrange("e a p n r -> a p e (n r)")
         for a in range(PASSES):
             nc.sync.dma_start(out=ww[:, a, :, :], in_=w_view[a])
         nc.sync.dma_start(out=pos1_sb[:], in_=pos1)
         nc.sync.dma_start(out=pos2_sb[:], in_=pos2)
-        gates = keep.tile([P, 2, T], F32, name="gates")
+        gates = keep.tile([P, 2, T], F32, name="gates", align_bytes=256)
         nc.sync.dma_start(out=gates[:], in_=gate.rearrange("s n t -> n s t"))
 
-        words_slot = keep.tile([P, PASSES, SLOTS], U32, name="words_slot", align_bytes=64)
-        bytes_slot = keep.tile([P, SLOTS], U8, name="bytes_slot", align_bytes=64)
+        words_slot = keep.tile([P, PASSES, SLOTS], U32, name="words_slot", align_bytes=256)
+        bytes_slot = keep.tile([P, SLOTS], U8, name="bytes_slot", align_bytes=256)
 
         def gather(dst, window, idx, lo, hi):
             nc.vector.tensor_copy(out=dst[:, lo:hi], in_=window[:, : max(T, (hi - lo) * 11 // 8)].indirect(idx[:, lo // 16 : hi // 16]))
 
-        grouped = [keep.tile([P, T, 4], BF16, name="grouped%d" % a, align_bytes=64) for a in range(PASSES)]
+        grouped = [keep.tile([P, T, 4], BF16, name="grouped%d" % a, align_bytes=256) for a in range(PASSES)]
 
         def interleave(copy, a, lo, hi):
             start = lo // LOAD * LOAD
@@ -102,7 +102,7 @@ def tile_routed_moe_kernel(tc, xT, w_words, w_scales, gate, offs, pos1, pos2, ou
         quantise(1, 0, 256)
         quantise(1, 256, 512)
 
-        y = keep.tile([P, SLOTS], F32, name="y")
+        y = keep.tile([P, SLOTS], F32, name="y", align_bytes=256)
 
         def multiply(bank, e, a):
             cols = slice(e * C, (e + 1) * C)
@@ -129,18 +129,18 @@ def tile_routed_moe_kernel(tc, xT, w_words, w_scales, gate, offs, pos1, pos2, ou
             copy = nc.vector.tensor_copy if e in (E - 3, E - 2) else nc.scalar.copy
             copy(out=y[:, e * C : (e + 1) * C], in_=sums[e][:])
 
-        first = keep.tile([N, T], F32, name="first")
+        first = keep.tile([N, T], F32, name="first", align_bytes=256)
         nc.vector.tensor_tensor(first[:], y[:].indirect(pos1_sb[:]), gates[:, 0, :], MULT)
         pieces = list(zip(OUT_CUTS, OUT_CUTS[1:]))
         seconds = {}
 
         def finish(lo, hi):
-            total = keep.tile([N, hi - lo], F32, name="total%d" % lo)
+            total = keep.tile([N, hi - lo], F32, name="total%d" % lo, align_bytes=256)
             nc.vector.tensor_tensor(total[:], first[:, lo:hi], seconds[lo][:], ADD)
             nc.sync.dma_start(out=out[:, lo:hi], in_=total[:])
 
         for lo, hi in pieces:
-            second = keep.tile([N, hi - lo], F32, name="second%d" % lo)
+            second = keep.tile([N, hi - lo], F32, name="second%d" % lo, align_bytes=256)
             nc.vector.tensor_tensor(second[:], y[:].indirect(pos2_sb[:, lo // 16 : hi // 16]), gates[:, 1, lo:hi], MULT)
             seconds[lo] = second
         for lo, hi in pieces:

@@ -20,7 +20,7 @@ ADD = mybir.AluOpType.add
 
 WORD_WINDOWS = (1408, 880)
 BYTE_WINDOW = 1408
-LOAD = 256
+LOADS = ((0, 256, 384, 512), (0, 256, 512))
 WORD1_CUTS = (0, 640, 896, 1024)
 OUT_CUTS = (0, 256, 512)
 
@@ -49,8 +49,7 @@ def tile_routed_moe_kernel(tc, xT, w_words, w_scales, gate, offs, pos1, pos2, ou
         raw = {}
         x_view = xT.rearrange("(a p j) t -> a p j t", p=P, j=4)
         for a in range(PASSES):
-            for lo in range(0, T, LOAD):
-                hi = lo + LOAD
+            for lo, hi in zip(LOADS[a], LOADS[a][1:]):
                 chunk = keep.tile([P, 4, hi - lo], F32, name="raw%d_%d" % (a, lo), align_bytes=256)
                 nc.sync.dma_start(out=chunk[:], in_=x_view[a, :, :, lo:hi])
                 raw[a, lo] = chunk
@@ -59,10 +58,8 @@ def tile_routed_moe_kernel(tc, xT, w_words, w_scales, gate, offs, pos1, pos2, ou
         s_view = w_scales.rearrange("e a q n -> q (e a) n")
         for q in range(4):
             nc.sync.dma_start(out=ws[32 * q : 32 * q + 4, :, :].bitcast(I32), in_=s_view[4 * q : 4 * q + 4, :, :].bitcast(I32))
-        ww = keep.tile([P, PASSES, E, 4 * N], U8, name="ww", align_bytes=256)
-        w_view = w_words.rearrange("e a p n r -> a p e (n r)")
-        for a in range(PASSES):
-            nc.sync.dma_start(out=ww[:, a, :, :], in_=w_view[a])
+        ww = keep.tile([P, E * PASSES, 4 * N], U8, name="ww", align_bytes=256)
+        nc.sync.dma_start(out=ww[:], in_=w_words.rearrange("e a p n r -> p (e a) (n r)"))
         nc.sync.dma_start(out=pos1_sb[:], in_=pos1)
         nc.sync.dma_start(out=pos2_sb[:], in_=pos2)
         gates = keep.tile([P, 2, T], F32, name="gates", align_bytes=256)
@@ -77,7 +74,7 @@ def tile_routed_moe_kernel(tc, xT, w_words, w_scales, gate, offs, pos1, pos2, ou
         grouped = [keep.tile([P, T, 4], BF16, name="grouped%d" % a, align_bytes=256) for a in range(PASSES)]
 
         def interleave(copy, a, lo, hi):
-            start = lo // LOAD * LOAD
+            start = max(cut for cut in LOADS[a] if cut <= lo)
             dst = grouped[a][:, lo:hi, :].rearrange("p (b i) j -> p b j i", i=4)
             src = raw[a, start][:, :, lo - start : hi - start].rearrange("p j (b i) -> p b j i", i=4)
             copy(out=dst, in_=src)
@@ -92,13 +89,16 @@ def tile_routed_moe_kernel(tc, xT, w_words, w_scales, gate, offs, pos1, pos2, ou
         interleave(nc.scalar.copy, 0, 176, 256)
         interleave(nc.vector.tensor_copy, 0, 0, 176)
         quantise(0, 0, 256)
-        interleave(nc.scalar.copy, 0, 432, 512)
-        interleave(nc.vector.tensor_copy, 0, 256, 432)
-        quantise(0, 256, 512)
+        interleave(nc.scalar.copy, 0, 320, 384)
+        interleave(nc.vector.tensor_copy, 0, 256, 320)
+        interleave(nc.scalar.copy, 0, 472, 512)
+        interleave(nc.vector.tensor_copy, 0, 384, 472)
+        quantise(0, 256, 384)
+        quantise(0, 384, 512)
         gather(words_slot[:, 0, :], words_all[0], offs_sb, 0, 1024)
         interleave(nc.scalar.copy, 1, 0, 256)
-        interleave(nc.scalar.copy, 1, 288, 512)
-        interleave(nc.vector.tensor_copy, 1, 256, 288)
+        interleave(nc.scalar.copy, 1, 320, 512)
+        interleave(nc.vector.tensor_copy, 1, 256, 320)
         quantise(1, 0, 256)
         quantise(1, 256, 512)
 
@@ -108,7 +108,7 @@ def tile_routed_moe_kernel(tc, xT, w_words, w_scales, gate, offs, pos1, pos2, ou
             cols = slice(e * C, (e + 1) * C)
             nc.tensor.matmul_mx(
                 out=bank,
-                lhsT=ww[:, a, e, :].bitcast(FP8X4),
+                lhsT=ww[:, e * PASSES + a, :].bitcast(FP8X4),
                 lhsT_scale=ws[:, e * PASSES + a, :],
                 rhs=words_slot[:, a, cols].bitcast(FP8X4),
                 rhs_scale=bytes_slot[4 * a :, cols],

@@ -19,9 +19,10 @@ MULT = mybir.AluOpType.mult
 ADD = mybir.AluOpType.add
 
 WORD_WINDOWS = (1408, 880)
-BYTE_WINDOW = 1408
-LOADS = ((0, 256, 384, 512), (0, 256, 512))
+BYTE_WINDOW = 1056
+LOADS = ((0, 256, 384, 512), (0, 128, 256, 384, 512))
 WORD1_CUTS = (0, 640, 896, 1024)
+W_LOADS = ((0, 0, 4), (0, 4, 8), (1, 0, 4), (1, 4, 8))
 OUT_CUTS = (0, 256, 512)
 
 
@@ -58,12 +59,15 @@ def tile_routed_moe_kernel(tc, xT, w_words, w_scales, gate, offs, pos1, pos2, ou
         s_view = w_scales.rearrange("e a q n -> q (e a) n")
         for q in range(4):
             nc.sync.dma_start(out=ws[32 * q : 32 * q + 4, :, :].bitcast(I32), in_=s_view[4 * q : 4 * q + 4, :, :].bitcast(I32))
-        ww = keep.tile([P, E * PASSES, 4 * N], U8, name="ww", align_bytes=256)
-        nc.sync.dma_start(out=ww[:], in_=w_words.rearrange("e a p n r -> p (e a) (n r)"))
-        nc.sync.dma_start(out=pos1_sb[:], in_=pos1)
-        nc.sync.dma_start(out=pos2_sb[:], in_=pos2)
+        ww = keep.tile([P, PASSES, E, 4 * N], U8, name="ww", align_bytes=256)
+        w_view = w_words.rearrange("e a p n r -> a p e (n r)")
+        for a, lo, hi in W_LOADS:
+            nc.sync.dma_start(out=ww[:, a, lo:hi, :], in_=w_view[a, :, lo:hi, :])
         gates = keep.tile([P, 2, T], F32, name="gates", align_bytes=256)
-        nc.sync.dma_start(out=gates[:], in_=gate.rearrange("s n t -> n s t"))
+        nc.sync.dma_start(out=pos1_sb[:], in_=pos1)
+        nc.sync.dma_start(out=gates[:, 0, :], in_=gate[0])
+        nc.sync.dma_start(out=pos2_sb[:], in_=pos2)
+        nc.sync.dma_start(out=gates[:, 1, :], in_=gate[1])
 
         words_slot = keep.tile([P, PASSES, SLOTS], U32, name="words_slot", align_bytes=256)
         bytes_slot = keep.tile([P, SLOTS], U8, name="bytes_slot", align_bytes=256)
@@ -86,19 +90,19 @@ def tile_routed_moe_kernel(tc, xT, w_words, w_scales, gate, offs, pos1, pos2, ou
                 in_=grouped[a][:, lo:hi, :].rearrange("p t j -> p (t j)"),
             )
 
-        interleave(nc.scalar.copy, 0, 176, 256)
-        interleave(nc.vector.tensor_copy, 0, 0, 176)
+        interleave(nc.scalar.copy, 0, 160, 256)
+        interleave(nc.vector.tensor_copy, 0, 0, 160)
         quantise(0, 0, 256)
-        interleave(nc.scalar.copy, 0, 320, 384)
-        interleave(nc.vector.tensor_copy, 0, 256, 320)
+        interleave(nc.scalar.copy, 0, 256, 384)
         interleave(nc.scalar.copy, 0, 472, 512)
         interleave(nc.vector.tensor_copy, 0, 384, 472)
         quantise(0, 256, 384)
         quantise(0, 384, 512)
         gather(words_slot[:, 0, :], words_all[0], offs_sb, 0, 1024)
-        interleave(nc.scalar.copy, 1, 0, 256)
-        interleave(nc.scalar.copy, 1, 320, 512)
-        interleave(nc.vector.tensor_copy, 1, 256, 320)
+        interleave(nc.scalar.copy, 1, 0, 128)
+        interleave(nc.scalar.copy, 1, 128, 256)
+        interleave(nc.scalar.copy, 1, 256, 384)
+        interleave(nc.scalar.copy, 1, 384, 512)
         quantise(1, 0, 256)
         quantise(1, 256, 512)
 
@@ -108,7 +112,7 @@ def tile_routed_moe_kernel(tc, xT, w_words, w_scales, gate, offs, pos1, pos2, ou
             cols = slice(e * C, (e + 1) * C)
             nc.tensor.matmul_mx(
                 out=bank,
-                lhsT=ww[:, e * PASSES + a, :].bitcast(FP8X4),
+                lhsT=ww[:, a, e, :].bitcast(FP8X4),
                 lhsT_scale=ws[:, e * PASSES + a, :],
                 rhs=words_slot[:, a, cols].bitcast(FP8X4),
                 rhs_scale=bytes_slot[4 * a :, cols],

@@ -18,11 +18,15 @@ FP8X4 = mybir.dt.float8_e4m3fn_x4
 MULT = mybir.AluOpType.mult
 ADD = mybir.AluOpType.add
 
-WORD_WINDOWS = (1408, 880)
-BYTE_WINDOW = 1056
+WORD_WINDOWS = (1408, 896)
+BYTE_WINDOW = 1408
 LOADS = ((0, 256, 384, 512), (0, 128, 256, 384, 512))
+BYTE_CUTS = (0, 1024)
 WORD1_CUTS = (0, 640, 896, 1024)
+BANKS = ((0, 3), (3, 5), (5, 7), (7, 8))
+VECTOR_BANKS = (2,)
 W_LOADS = ((0, 0, 4), (0, 4, 8), (1, 0, 4), (1, 4, 8))
+SECOND_CUTS = (0, 256, 512)
 OUT_CUTS = (0, 256, 512)
 
 
@@ -37,15 +41,15 @@ def tile_routed_moe_kernel(tc, xT, w_words, w_scales, gate, offs, pos1, pos2, ou
         pos1_sb = lists.tile([P, T // 16], U16, name="pos1_sb")
         pos2_sb = lists.tile([P, T // 16], U16, name="pos2_sb")
 
+        ws = keep.tile([P, E * PASSES, N], U8, name="ws", align_bytes=256)
+        nc.vector.memset(ws[:].rearrange("p b n -> p (b n)").bitcast(I32), 0)
+        bytes_all = keep.tile([P, BYTE_WINDOW], U8, name="bytes_all", align_bytes=256)
+        nc.vector.memset(bytes_all[:].bitcast(I32), 0)
         words_all = []
         for a in range(PASSES):
             words = keep.tile([P, WORD_WINDOWS[a]], U32, name="words_all%d" % a, align_bytes=256)
             nc.vector.memset(words[:, T:].bitcast(I32), 0)
             words_all.append(words)
-        bytes_all = keep.tile([P, BYTE_WINDOW], U8, name="bytes_all", align_bytes=256)
-        nc.gpsimd.memset(bytes_all[:].bitcast(I32), 0)
-        ws = keep.tile([P, E * PASSES, N], U8, name="ws", align_bytes=256)
-        nc.gpsimd.memset(ws[:].rearrange("p b n -> p (b n)").bitcast(I32), 0)
 
         raw = {}
         x_view = xT.rearrange("(a p j) t -> a p j t", p=P, j=4)
@@ -98,54 +102,47 @@ def tile_routed_moe_kernel(tc, xT, w_words, w_scales, gate, offs, pos1, pos2, ou
         interleave(nc.vector.tensor_copy, 0, 384, 472)
         quantise(0, 256, 384)
         quantise(0, 384, 512)
-        gather(words_slot[:, 0, :], words_all[0], offs_sb, 0, 1024)
-        interleave(nc.scalar.copy, 1, 0, 128)
-        interleave(nc.scalar.copy, 1, 128, 256)
-        interleave(nc.scalar.copy, 1, 256, 384)
-        interleave(nc.scalar.copy, 1, 384, 512)
+        gather(words_slot[:, 0, :], words_all[0], offs_sb, 0, SLOTS)
+        for lo, hi in zip(LOADS[1], LOADS[1][1:]):
+            interleave(nc.scalar.copy, 1, lo, hi)
         quantise(1, 0, 256)
         quantise(1, 256, 512)
 
         y = keep.tile([P, SLOTS], F32, name="y", align_bytes=256)
+        sums = [psum.tile([N, (hi - lo) * C], F32, name="sums%d" % lo) for lo, hi in BANKS]
 
-        def multiply(bank, e, a):
+        def multiply(e, a):
+            b = max(i for i, (lo, hi) in enumerate(BANKS) if lo <= e)
+            lo, hi = BANKS[b]
             cols = slice(e * C, (e + 1) * C)
             nc.tensor.matmul_mx(
-                out=bank,
+                out=sums[b][:, (e - lo) * C : (e - lo + 1) * C],
                 lhsT=ww[:, a, e, :].bitcast(FP8X4),
                 lhsT_scale=ws[:, e * PASSES + a, :],
                 rhs=words_slot[:, a, cols].bitcast(FP8X4),
                 rhs_scale=bytes_slot[4 * a :, cols],
-                start=(a == 0),
-                stop=(a == PASSES - 1),
+                start=(a == 0 and e == lo),
+                stop=(a == PASSES - 1 and e == hi - 1),
             )
 
-        gather(bytes_slot, bytes_all, offs_sb, 0, 3 * SLOTS // 4)
-        gather(bytes_slot, bytes_all, offs_sb, 3 * SLOTS // 4, SLOTS)
-        sums = [psum.tile([N, C], F32, name="sums%d" % e) for e in range(E)]
+        for lo, hi in zip(BYTE_CUTS, BYTE_CUTS[1:]):
+            gather(bytes_slot, bytes_all, offs_sb, lo, hi)
         for e in range(E):
-            multiply(sums[e][:], e, 0)
+            multiply(e, 0)
         for lo, hi in zip(WORD1_CUTS, WORD1_CUTS[1:]):
             gather(words_slot[:, 1, :], words_all[1], offs_sb, lo, hi)
             for e in range(lo // C, hi // C):
-                multiply(sums[e][:], e, 1)
-        for e in range(E):
-            copy = nc.vector.tensor_copy if e in (E - 3, E - 2) else nc.scalar.copy
-            copy(out=y[:, e * C : (e + 1) * C], in_=sums[e][:])
+                multiply(e, 1)
+        for b, (lo, hi) in enumerate(BANKS):
+            copy = nc.vector.tensor_copy if b in VECTOR_BANKS else nc.scalar.copy
+            copy(out=y[:, lo * C : hi * C], in_=sums[b][:])
 
         first = keep.tile([N, T], F32, name="first", align_bytes=256)
+        second = keep.tile([N, T], F32, name="second", align_bytes=256)
         nc.vector.tensor_tensor(first[:], y[:].indirect(pos1_sb[:]), gates[:, 0, :], MULT)
-        pieces = list(zip(OUT_CUTS, OUT_CUTS[1:]))
-        seconds = {}
-
-        def finish(lo, hi):
+        for lo, hi in zip(SECOND_CUTS, SECOND_CUTS[1:]):
+            nc.vector.tensor_tensor(second[:, lo:hi], y[:].indirect(pos2_sb[:, lo // 16 : hi // 16]), gates[:, 1, lo:hi], MULT)
+        for lo, hi in zip(OUT_CUTS, OUT_CUTS[1:]):
             total = keep.tile([N, hi - lo], F32, name="total%d" % lo, align_bytes=256)
-            nc.vector.tensor_tensor(total[:], first[:, lo:hi], seconds[lo][:], ADD)
+            nc.vector.tensor_tensor(total[:], first[:, lo:hi], second[:, lo:hi], ADD)
             nc.sync.dma_start(out=out[:, lo:hi], in_=total[:])
-
-        for lo, hi in pieces:
-            second = keep.tile([N, hi - lo], F32, name="second%d" % lo, align_bytes=256)
-            nc.vector.tensor_tensor(second[:], y[:].indirect(pos2_sb[:, lo // 16 : hi // 16]), gates[:, 1, lo:hi], MULT)
-            seconds[lo] = second
-        for lo, hi in pieces:
-            finish(lo, hi)

@@ -1,3 +1,4 @@
+import math
 from contextlib import ExitStack
 
 import concourse.mybir as mybir
@@ -28,6 +29,7 @@ VECTOR_BANKS = (2,)
 W_LOADS = ((0, 0, 4), (0, 4, 8), (1, 0, 4), (1, 4, 8))
 SECOND_CUTS = (0, 256, 512)
 OUT_CUTS = (0, 256, 512)
+REGION = 32768
 
 
 def tile_routed_moe_kernel(tc, xT, w_words, w_scales, gate, offs, pos1, pos2, out):
@@ -41,13 +43,20 @@ def tile_routed_moe_kernel(tc, xT, w_words, w_scales, gate, offs, pos1, pos2, ou
         pos1_sb = lists.tile([P, T // 16], U16, name="pos1_sb")
         pos2_sb = lists.tile([P, T // 16], U16, name="pos2_sb")
 
-        ws = keep.tile([P, E * PASSES, N], U8, name="ws", align_bytes=256)
-        nc.vector.memset(ws[:].rearrange("p b n -> p (b n)").bitcast(I32), 0)
-        bytes_all = keep.tile([P, BYTE_WINDOW], U8, name="bytes_all", align_bytes=256)
-        nc.vector.memset(bytes_all[:].bitcast(I32), 0)
+        used = {}
+
+        def place(region, shape, dtype, size, name):
+            start = used.get(region, region * REGION)
+            used[region] = start + (size * math.prod(shape[1:]) + 255) // 256 * 256
+            return keep.tile(shape, dtype, name=name, align_bytes=256, offset=start)
+
+        ws = place(4, [P, E * PASSES, N], U8, 1, "ws")
+        nc.gpsimd.memset(ws[:].rearrange("p b n -> p (b n)").bitcast(I32), 0)
+        bytes_all = place(2, [P, BYTE_WINDOW], U8, 1, "bytes_all")
+        nc.gpsimd.memset(bytes_all[:].bitcast(I32), 0)
         words_all = []
         for a in range(PASSES):
-            words = keep.tile([P, WORD_WINDOWS[a]], U32, name="words_all%d" % a, align_bytes=256)
+            words = place(2, [P, WORD_WINDOWS[a]], U32, 4, "words_all%d" % a)
             nc.vector.memset(words[:, T:].bitcast(I32), 0)
             words_all.append(words)
 
@@ -55,7 +64,7 @@ def tile_routed_moe_kernel(tc, xT, w_words, w_scales, gate, offs, pos1, pos2, ou
         x_view = xT.rearrange("(a p j) t -> a p j t", p=P, j=4)
         for a in range(PASSES):
             for lo, hi in zip(LOADS[a], LOADS[a][1:]):
-                chunk = keep.tile([P, 4, hi - lo], F32, name="raw%d_%d" % (a, lo), align_bytes=256)
+                chunk = place(0, [P, 4, hi - lo], F32, 4, "raw%d_%d" % (a, lo))
                 nc.sync.dma_start(out=chunk[:], in_=x_view[a, :, :, lo:hi])
                 raw[a, lo] = chunk
             if a == 0:
@@ -63,23 +72,24 @@ def tile_routed_moe_kernel(tc, xT, w_words, w_scales, gate, offs, pos1, pos2, ou
         s_view = w_scales.rearrange("e a q n -> q (e a) n")
         for q in range(4):
             nc.sync.dma_start(out=ws[32 * q : 32 * q + 4, :, :].bitcast(I32), in_=s_view[4 * q : 4 * q + 4, :, :].bitcast(I32))
-        ww = keep.tile([P, PASSES, E, 4 * N], U8, name="ww", align_bytes=256)
+        ww = place(4, [P, PASSES, E, 4 * N], U8, 1, "ww")
         w_view = w_words.rearrange("e a p n r -> a p e (n r)")
         for a, lo, hi in W_LOADS:
             nc.sync.dma_start(out=ww[:, a, lo:hi, :], in_=w_view[a, :, lo:hi, :])
-        gates = keep.tile([P, 2, T], F32, name="gates", align_bytes=256)
+        gates = place(6, [P, 2, T], F32, 4, "gates")
         nc.sync.dma_start(out=pos1_sb[:], in_=pos1)
-        nc.sync.dma_start(out=gates[:, 0, :], in_=gate[0])
+        for lo, hi in zip(OUT_CUTS, OUT_CUTS[1:]):
+            nc.sync.dma_start(out=gates[:, 0, lo:hi], in_=gate[0, :, lo:hi])
         nc.sync.dma_start(out=pos2_sb[:], in_=pos2)
         nc.sync.dma_start(out=gates[:, 1, :], in_=gate[1])
 
-        words_slot = keep.tile([P, PASSES, SLOTS], U32, name="words_slot", align_bytes=256)
-        bytes_slot = keep.tile([P, SLOTS], U8, name="bytes_slot", align_bytes=256)
+        words_slot = place(3, [P, PASSES, SLOTS], U32, 4, "words_slot")
+        bytes_slot = place(3, [P, SLOTS], U8, 1, "bytes_slot")
 
         def gather(dst, window, idx, lo, hi):
             nc.vector.tensor_copy(out=dst[:, lo:hi], in_=window[:, : max(T, (hi - lo) * 11 // 8)].indirect(idx[:, lo // 16 : hi // 16]))
 
-        grouped = [keep.tile([P, T, 4], BF16, name="grouped%d" % a, align_bytes=256) for a in range(PASSES)]
+        grouped = [place(1, [P, T, 4], BF16, 2, "grouped%d" % a) for a in range(PASSES)]
 
         def interleave(copy, a, lo, hi):
             start = max(cut for cut in LOADS[a] if cut <= lo)
@@ -97,9 +107,10 @@ def tile_routed_moe_kernel(tc, xT, w_words, w_scales, gate, offs, pos1, pos2, ou
         interleave(nc.scalar.copy, 0, 160, 256)
         interleave(nc.vector.tensor_copy, 0, 0, 160)
         quantise(0, 0, 256)
-        interleave(nc.scalar.copy, 0, 256, 384)
-        interleave(nc.scalar.copy, 0, 472, 512)
-        interleave(nc.vector.tensor_copy, 0, 384, 472)
+        interleave(nc.scalar.copy, 0, 320, 384)
+        interleave(nc.vector.tensor_copy, 0, 256, 320)
+        interleave(nc.scalar.copy, 0, 448, 512)
+        interleave(nc.vector.tensor_copy, 0, 384, 448)
         quantise(0, 256, 384)
         quantise(0, 384, 512)
         gather(words_slot[:, 0, :], words_all[0], offs_sb, 0, SLOTS)
@@ -108,7 +119,7 @@ def tile_routed_moe_kernel(tc, xT, w_words, w_scales, gate, offs, pos1, pos2, ou
         quantise(1, 0, 256)
         quantise(1, 256, 512)
 
-        y = keep.tile([P, SLOTS], F32, name="y", align_bytes=256)
+        y = place(5, [P, SLOTS], F32, 4, "y")
         sums = [psum.tile([N, (hi - lo) * C], F32, name="sums%d" % lo) for lo, hi in BANKS]
 
         def multiply(e, a):
@@ -137,12 +148,12 @@ def tile_routed_moe_kernel(tc, xT, w_words, w_scales, gate, offs, pos1, pos2, ou
             copy = nc.vector.tensor_copy if b in VECTOR_BANKS else nc.scalar.copy
             copy(out=y[:, lo * C : hi * C], in_=sums[b][:])
 
-        first = keep.tile([N, T], F32, name="first", align_bytes=256)
-        second = keep.tile([N, T], F32, name="second", align_bytes=256)
+        first = place(1, [N, T], F32, 4, "first")
+        second = place(2, [N, T], F32, 4, "second")
         nc.vector.tensor_tensor(first[:], y[:].indirect(pos1_sb[:]), gates[:, 0, :], MULT)
         for lo, hi in zip(SECOND_CUTS, SECOND_CUTS[1:]):
             nc.vector.tensor_tensor(second[:, lo:hi], y[:].indirect(pos2_sb[:, lo // 16 : hi // 16]), gates[:, 1, lo:hi], MULT)
         for lo, hi in zip(OUT_CUTS, OUT_CUTS[1:]):
-            total = keep.tile([N, hi - lo], F32, name="total%d" % lo, align_bytes=256)
+            total = place(0, [N, hi - lo], F32, 4, "total%d" % lo)
             nc.vector.tensor_tensor(total[:], first[:, lo:hi], second[:, lo:hi], ADD)
             nc.sync.dma_start(out=out[:, lo:hi], in_=total[:])

@@ -26,7 +26,7 @@ BYTE_CUTS = (0, 1024)
 WORD1_CUTS = (0, 640, 896, 1024)
 BANKS = ((0, 3), (3, 5), (5, 7), (7, 8))
 VECTOR_BANKS = (2,)
-W_LOADS = ((0, 0, 4), (0, 4, 8), (1, 0, 4), (1, 4, 8))
+W_LOADS = ((0, 0, 4), (0, 4, 8), (1, 0, 4), (1, 4, 6), (1, 6, 8))
 SECOND_CUTS = (0, 256, 512)
 OUT_CUTS = (0, 256, 512)
 REGION = 32768

@@ -20,13 +20,13 @@ MULT = mybir.AluOpType.mult
 ADD = mybir.AluOpType.add
 
 WORD_WINDOWS = (1408, 896)
-BYTE_WINDOW = 1408
+BYTE_WINDOW = 896
 LOADS = ((0, 256, 384, 512), (0, 128, 256, 384, 512))
-BYTE_CUTS = (0, 1024)
+BYTE_CUTS = (0, 640, 1024)
 WORD1_CUTS = (0, 640, 896, 1024)
 BANKS = ((0, 3), (3, 5), (5, 7), (7, 8))
 VECTOR_BANKS = (2,)
-W_LOADS = ((0, 0, 4), (0, 4, 8), (1, 0, 4), (1, 4, 6), (1, 6, 8))
+W_LOADS = ((0, 0, 5), (1, 0, 5), (0, 5, 8), (1, 5, 7), (1, 7, 8))
 SECOND_CUTS = (0, 256, 512)
 OUT_CUTS = (0, 256, 512)
 REGION = 32768
@@ -136,11 +136,12 @@ def tile_routed_moe_kernel(tc, xT, w_words, w_scales, gate, offs, pos1, pos2, ou
                 stop=(a == PASSES - 1 and e == hi - 1),
             )
 
-        for lo, hi in zip(BYTE_CUTS, BYTE_CUTS[1:]):
-            gather(bytes_slot, bytes_all, offs_sb, lo, hi)
-        for e in range(E):
-            multiply(e, 0)
+        byte_ends = dict(zip(BYTE_CUTS, BYTE_CUTS[1:]))
         for lo, hi in zip(WORD1_CUTS, WORD1_CUTS[1:]):
+            if lo in byte_ends:
+                gather(bytes_slot, bytes_all, offs_sb, lo, byte_ends[lo])
+                for e in range(lo // C, byte_ends[lo] // C):
+                    multiply(e, 0)
             gather(words_slot[:, 1, :], words_all[1], offs_sb, lo, hi)
             for e in range(lo // C, hi // C):
                 multiply(e, 1)

@@ -24,8 +24,7 @@ BYTE_WINDOW = 896
 LOADS = ((0, 256, 384, 512), (0, 128, 256, 384, 512))
 BYTE_CUTS = (0, 640, 1024)
 WORD1_CUTS = (0, 640, 896, 1024)
-BANKS = ((0, 3), (3, 5), (5, 7), (7, 8))
-VECTOR_BANKS = (2,)
+BANKS = ((0, 3), (3, 5), (5, 6), (6, 7), (7, 8))
 W_LOADS = ((0, 0, 5), (1, 0, 5), (0, 5, 8), (1, 5, 7), (1, 7, 8))
 SECOND_CUTS = (0, 256, 512)
 OUT_CUTS = (0, 256, 512)
@@ -146,8 +145,7 @@ def tile_routed_moe_kernel(tc, xT, w_words, w_scales, gate, offs, pos1, pos2, ou
             for e in range(lo // C, hi // C):
                 multiply(e, 1)
         for b, (lo, hi) in enumerate(BANKS):
-            copy = nc.vector.tensor_copy if b in VECTOR_BANKS else nc.scalar.copy
-            copy(out=y[:, lo * C : hi * C], in_=sums[b][:])
+            nc.scalar.copy(out=y[:, lo * C : hi * C], in_=sums[b][:])
 
         first = place(1, [N, T], F32, 4, "first")
         second = place(2, [N, T], F32, 4, "second")

@@ -19,16 +19,17 @@ FP8X4 = mybir.dt.float8_e4m3fn_x4
 MULT = mybir.AluOpType.mult
 ADD = mybir.AluOpType.add
 
-WORD_WINDOWS = (1408, 896)
-BYTE_WINDOW = 896
+WORD_WINDOWS = (1248, 704)
+BYTE_WINDOW = 1248
 LOADS = ((0, 256, 384, 512), (0, 128, 256, 384, 512))
-BYTE_CUTS = (0, 640, 1024)
-WORD1_CUTS = (0, 640, 896, 1024)
-BANKS = ((0, 3), (3, 5), (5, 6), (6, 7), (7, 8))
-W_LOADS = ((0, 0, 5), (1, 0, 5), (0, 5, 8), (1, 5, 7), (1, 7, 8))
+BYTE_CUTS = (0, 896, 1024)
+WORD1_CUTS = (0, 512, 896, 1024)
+BANKS = ((0, 2), (2, 4), (4, 5), (5, 6), (6, 7), (7, 8))
+W_LOADS = ((0, 0, 4), (0, 4, 7), (1, 0, 4), (1, 4, 7), (0, 7, 8), (1, 7, 8))
 SECOND_CUTS = (0, 256, 512)
 OUT_CUTS = (0, 256, 512)
 REGION = 32768
+HALF = T // 2
 
 
 def tile_routed_moe_kernel(tc, xT, w_words, w_scales, gate, offs, pos1, pos2, out):
@@ -77,8 +78,7 @@ def tile_routed_moe_kernel(tc, xT, w_words, w_scales, gate, offs, pos1, pos2, ou
             nc.sync.dma_start(out=ww[:, a, lo:hi, :], in_=w_view[a, :, lo:hi, :])
         gates = place(6, [P, 2, T], F32, 4, "gates")
         nc.sync.dma_start(out=pos1_sb[:], in_=pos1)
-        for lo, hi in zip(OUT_CUTS, OUT_CUTS[1:]):
-            nc.sync.dma_start(out=gates[:, 0, lo:hi], in_=gate[0, :, lo:hi])
+        nc.sync.dma_start(out=gates[:, 0, :], in_=gate[0])
         nc.sync.dma_start(out=pos2_sb[:], in_=pos2)
         nc.sync.dma_start(out=gates[:, 1, :], in_=gate[1])
 
@@ -86,13 +86,17 @@ def tile_routed_moe_kernel(tc, xT, w_words, w_scales, gate, offs, pos1, pos2, ou
         bytes_slot = place(3, [P, SLOTS], U8, 1, "bytes_slot")
 
         def gather(dst, window, idx, lo, hi):
-            nc.vector.tensor_copy(out=dst[:, lo:hi], in_=window[:, : max(T, (hi - lo) * 11 // 8)].indirect(idx[:, lo // 16 : hi // 16]))
+            nc.vector.tensor_copy(out=dst, in_=window[:, : max(T, (hi - lo) * 11 // 8)].indirect(idx[:, lo // 16 : hi // 16]))
 
-        grouped = [place(1, [P, T, 4], BF16, 2, "grouped%d" % a) for a in range(PASSES)]
+        grouped = {(a, lo): place(1, [P, HALF, 4], BF16, 2, "grouped%d_%d" % (a, lo)) for a in range(PASSES) for lo in (0, HALF)}
+
+        def rows(a, lo, hi):
+            start = lo // HALF * HALF
+            return grouped[a, start][:, lo - start : hi - start, :]
 
         def interleave(copy, a, lo, hi):
             start = max(cut for cut in LOADS[a] if cut <= lo)
-            dst = grouped[a][:, lo:hi, :].rearrange("p (b i) j -> p b j i", i=4)
+            dst = rows(a, lo, hi).rearrange("p (b i) j -> p b j i", i=4)
             src = raw[a, start][:, :, lo - start : hi - start].rearrange("p j (b i) -> p b j i", i=4)
             copy(out=dst, in_=src)
 
@@ -100,7 +104,7 @@ def tile_routed_moe_kernel(tc, xT, w_words, w_scales, gate, offs, pos1, pos2, ou
             nc.vector.quantize_mx(
                 out=words_all[a][:, lo:hi].bitcast(FP8X4),
                 scales=bytes_all[4 * a :, lo:hi],
-                in_=grouped[a][:, lo:hi, :].rearrange("p t j -> p (t j)"),
+                in_=rows(a, lo, hi).rearrange("p t j -> p (t j)"),
             )
 
         interleave(nc.scalar.copy, 0, 160, 256)
@@ -112,11 +116,14 @@ def tile_routed_moe_kernel(tc, xT, w_words, w_scales, gate, offs, pos1, pos2, ou
         interleave(nc.vector.tensor_copy, 0, 384, 448)
         quantise(0, 256, 384)
         quantise(0, 384, 512)
-        gather(words_slot[:, 0, :], words_all[0], offs_sb, 0, SLOTS)
+        gather(words_slot[:, 0, : SLOTS - C], words_all[0], offs_sb, 0, SLOTS - C)
         for lo, hi in zip(LOADS[1], LOADS[1][1:]):
             interleave(nc.scalar.copy, 1, lo, hi)
         quantise(1, 0, 256)
-        quantise(1, 256, 512)
+        quantise(1, 256, 384)
+        quantise(1, 384, 512)
+        words_last = keep.tile([P, C], U32, name="words_last", align_bytes=256, offset=(2 * T - 128) * 16)
+        gather(words_last[:], words_all[0], offs_sb, SLOTS - C, SLOTS)
 
         y = place(5, [P, SLOTS], F32, 4, "y")
         sums = [psum.tile([N, (hi - lo) * C], F32, name="sums%d" % lo) for lo, hi in BANKS]
@@ -129,7 +136,7 @@ def tile_routed_moe_kernel(tc, xT, w_words, w_scales, gate, offs, pos1, pos2, ou
                 out=sums[b][:, (e - lo) * C : (e - lo + 1) * C],
                 lhsT=ww[:, a, e, :].bitcast(FP8X4),
                 lhsT_scale=ws[:, e * PASSES + a, :],
-                rhs=words_slot[:, a, cols].bitcast(FP8X4),
+                rhs=(words_last[:] if (e, a) == (E - 1, 0) else words_slot[:, a, cols]).bitcast(FP8X4),
                 rhs_scale=bytes_slot[4 * a :, cols],
                 start=(a == 0 and e == lo),
                 stop=(a == PASSES - 1 and e == hi - 1),
@@ -138,10 +145,10 @@ def tile_routed_moe_kernel(tc, xT, w_words, w_scales, gate, offs, pos1, pos2, ou
         byte_ends = dict(zip(BYTE_CUTS, BYTE_CUTS[1:]))
         for lo, hi in zip(WORD1_CUTS, WORD1_CUTS[1:]):
             if lo in byte_ends:
-                gather(bytes_slot, bytes_all, offs_sb, lo, byte_ends[lo])
+                gather(bytes_slot[:, lo : byte_ends[lo]], bytes_all, offs_sb, lo, byte_ends[lo])
                 for e in range(lo // C, byte_ends[lo] // C):
                     multiply(e, 0)
-            gather(words_slot[:, 1, :], words_all[1], offs_sb, lo, hi)
+            gather(words_slot[:, 1, lo:hi], words_all[1], offs_sb, lo, hi)
             for e in range(lo // C, hi // C):
                 multiply(e, 1)
         for b, (lo, hi) in enumerate(BANKS):

@@ -18,6 +18,7 @@ U8 = mybir.dt.uint8
 FP8X4 = mybir.dt.float8_e4m3fn_x4
 MULT = mybir.AluOpType.mult
 ADD = mybir.AluOpType.add
+COPY = mybir.ActivationFunctionType.Copy
 
 WORD_WINDOWS = (1248, 704)
 BYTE_WINDOW = 1248
@@ -26,7 +27,6 @@ BYTE_CUTS = (0, 896, 1024)
 WORD1_CUTS = (0, 512, 896, 1024)
 BANKS = ((0, 2), (2, 4), (4, 5), (5, 6), (6, 7), (7, 8))
 W_LOADS = ((0, 0, 4), (0, 4, 7), (1, 0, 4), (1, 4, 7), (0, 7, 8), (1, 7, 8))
-SECOND_CUTS = (0, 256, 512)
 OUT_CUTS = (0, 256, 512)
 REGION = 32768
 HALF = T // 2
@@ -155,11 +155,15 @@ def tile_routed_moe_kernel(tc, xT, w_words, w_scales, gate, offs, pos1, pos2, ou
             nc.scalar.copy(out=y[:, lo * C : hi * C], in_=sums[b][:])
 
         first = place(1, [N, T], F32, 4, "first")
+        fetched = place(3, [N, T], F32, 4, "fetched")
         second = place(2, [N, T], F32, 4, "second")
+        halves = list(zip(OUT_CUTS, OUT_CUTS[1:]))
+        for lo, hi in halves:
+            nc.scalar.activation(fetched[:, lo:hi], y[:].indirect(pos2_sb[:, lo // 16 : hi // 16]), COPY)
         nc.vector.tensor_tensor(first[:], y[:].indirect(pos1_sb[:]), gates[:, 0, :], MULT)
-        for lo, hi in zip(SECOND_CUTS, SECOND_CUTS[1:]):
-            nc.vector.tensor_tensor(second[:, lo:hi], y[:].indirect(pos2_sb[:, lo // 16 : hi // 16]), gates[:, 1, lo:hi], MULT)
-        for lo, hi in zip(OUT_CUTS, OUT_CUTS[1:]):
+        for lo, hi in halves:
+            nc.vector.tensor_tensor(second[:, lo:hi], fetched[:, lo:hi], gates[:, 1, lo:hi], MULT)
+        for lo, hi in halves:
             total = place(0, [N, hi - lo], F32, 4, "total%d" % lo)
             nc.vector.tensor_tensor(total[:], first[:, lo:hi], second[:, lo:hi], ADD)
             nc.sync.dma_start(out=out[:, lo:hi], in_=total[:])

@@ -26,8 +26,9 @@ LOADS = ((0, 256, 384, 512), (0, 128, 256, 384, 512))
 BYTE_CUTS = (0, 896, 1024)
 WORD1_CUTS = (0, 512, 896, 1024)
 BANKS = ((0, 2), (2, 4), (4, 5), (5, 6), (6, 7), (7, 8))
-W_LOADS = ((0, 0, 4), (0, 4, 7), (1, 0, 4), (1, 4, 7), (0, 7, 8), (1, 7, 8))
-OUT_CUTS = (0, 256, 512)
+W_LOADS = ((0, 0, 4), (0, 4, 7), (1, 0, 4), (1, 4, 7))
+SECOND_CUTS = (0, 320, 512)
+OUT_CUTS = (0, 256, 384, 512)
 REGION = 32768
 HALF = T // 2
 
@@ -76,6 +77,7 @@ def tile_routed_moe_kernel(tc, xT, w_words, w_scales, gate, offs, pos1, pos2, ou
         w_view = w_words.rearrange("e a p n r -> a p e (n r)")
         for a, lo, hi in W_LOADS:
             nc.sync.dma_start(out=ww[:, a, lo:hi, :], in_=w_view[a, :, lo:hi, :])
+        nc.sync.dma_start(out=ww[:, :, E - 1, :], in_=w_words[E - 1].rearrange("a p n r -> p a (n r)"))
         gates = place(6, [P, 2, T], F32, 4, "gates")
         nc.sync.dma_start(out=pos1_sb[:], in_=pos1)
         nc.sync.dma_start(out=gates[:, 0, :], in_=gate[0])
@@ -157,13 +159,13 @@ def tile_routed_moe_kernel(tc, xT, w_words, w_scales, gate, offs, pos1, pos2, ou
         first = place(1, [N, T], F32, 4, "first")
         fetched = place(3, [N, T], F32, 4, "fetched")
         second = place(2, [N, T], F32, 4, "second")
-        halves = list(zip(OUT_CUTS, OUT_CUTS[1:]))
+        halves = list(zip(SECOND_CUTS, SECOND_CUTS[1:]))
         for lo, hi in halves:
             nc.scalar.activation(fetched[:, lo:hi], y[:].indirect(pos2_sb[:, lo // 16 : hi // 16]), COPY)
         nc.vector.tensor_tensor(first[:], y[:].indirect(pos1_sb[:]), gates[:, 0, :], MULT)
         for lo, hi in halves:
             nc.vector.tensor_tensor(second[:, lo:hi], fetched[:, lo:hi], gates[:, 1, lo:hi], MULT)
-        for lo, hi in halves:
+        for lo, hi in zip(OUT_CUTS, OUT_CUTS[1:]):
             total = place(0, [N, hi - lo], F32, 4, "total%d" % lo)
             nc.vector.tensor_tensor(total[:], first[:, lo:hi], second[:, lo:hi], ADD)
             nc.sync.dma_start(out=out[:, lo:hi], in_=total[:])

@@ -7,6 +7,9 @@ K, T, E, C, N = 1024, 512, 8, 128, 128
 SLOTS = E * C
 PASSES = K // 512
 P = 128
+PACK = 4
+PER_COLUMN = 16
+LAST = E - 1
 FLOPS = 2 * K * SLOTS * N
 
 F32 = mybir.dt.float32
@@ -20,17 +23,26 @@ MULT = mybir.AluOpType.mult
 ADD = mybir.AluOpType.add
 COPY = mybir.ActivationFunctionType.Copy
 
-WORD_WINDOWS = (1248, 704)
-BYTE_WINDOW = 1248
-LOADS = ((0, 256, 384, 512), (0, 128, 256, 384, 512))
-BYTE_CUTS = (0, 896, 1024)
-WORD1_CUTS = (0, 512, 896, 1024)
+X_CUTS = ((0, 256, 384, 512), (0, 128, 256, 384, 512))
+VECTOR_SHARES = (160, 64, 64)
+QUANT_CUTS = (0, 256, 384, 512)
+BYTE_CUTS = (0, LAST * C, SLOTS)
+WORD1_CUTS = (0, 4 * C, LAST * C, SLOTS)
 BANKS = ((0, 2), (2, 4), (4, 5), (5, 6), (6, 7), (7, 8))
-W_LOADS = ((0, 0, 4), (0, 4, 7), (1, 0, 4), (1, 4, 7))
-SECOND_CUTS = (0, 320, 512)
-OUT_CUTS = (0, 256, 384, 512)
+W_CUTS = (0, 4, LAST)
+SECOND_CUTS = (0, 320, T)
+OUT_CUTS = (0, 256, 384, T)
 REGION = 32768
+ALIGN = 256
 HALF = T // 2
+
+
+def pieces(cuts):
+    return list(zip(cuts, cuts[1:]))
+
+
+def window_width(entries):
+    return max(T, entries * 11 // 8)
 
 
 def tile_routed_moe_kernel(tc, xT, w_words, w_scales, gate, offs, pos1, pos2, out):
@@ -40,132 +52,132 @@ def tile_routed_moe_kernel(tc, xT, w_words, w_scales, gate, offs, pos1, pos2, ou
         keep = ctx.enter_context(tc.tile_pool(name="keep", bufs=1))
         psum = ctx.enter_context(tc.psum_pool(name="psum", bufs=1))
 
-        offs_sb = lists.tile([P, SLOTS // 16], U16, name="offs_sb")
-        pos1_sb = lists.tile([P, T // 16], U16, name="pos1_sb")
-        pos2_sb = lists.tile([P, T // 16], U16, name="pos2_sb")
+        offs_sb = lists.tile([P, SLOTS // PER_COLUMN], U16, name="offs_sb")
+        pos1_sb = lists.tile([P, T // PER_COLUMN], U16, name="pos1_sb")
+        pos2_sb = lists.tile([P, T // PER_COLUMN], U16, name="pos2_sb")
 
-        used = {}
+        free = {}
 
-        def place(region, shape, dtype, size, name):
-            start = used.get(region, region * REGION)
-            used[region] = start + (size * math.prod(shape[1:]) + 255) // 256 * 256
-            return keep.tile(shape, dtype, name=name, align_bytes=256, offset=start)
+        def place(region, shape, dtype, itemsize, name):
+            start = free.get(region, region * REGION)
+            free[region] = start + (itemsize * math.prod(shape[1:]) + ALIGN - 1) // ALIGN * ALIGN
+            return keep.tile(shape, dtype, name=name, align_bytes=ALIGN, offset=start)
 
-        ws = place(4, [P, E * PASSES, N], U8, 1, "ws")
-        nc.gpsimd.memset(ws[:].rearrange("p b n -> p (b n)").bitcast(I32), 0)
-        bytes_all = place(2, [P, BYTE_WINDOW], U8, 1, "bytes_all")
-        nc.gpsimd.memset(bytes_all[:].bitcast(I32), 0)
-        words_all = []
-        for a in range(PASSES):
-            words = place(2, [P, WORD_WINDOWS[a]], U32, 4, "words_all%d" % a)
+        def entries(list_tile, lo, hi):
+            return list_tile[:, lo // PER_COLUMN : hi // PER_COLUMN]
+
+        w_bytes = place(4, [P, E * PASSES, N], U8, 1, "w_bytes")
+        nc.gpsimd.memset(w_bytes[:].rearrange("p b n -> p (b n)").bitcast(I32), 0)
+        token_bytes = place(2, [P, window_width(BYTE_CUTS[1])], U8, 1, "token_bytes")
+        nc.gpsimd.memset(token_bytes[:].bitcast(I32), 0)
+        token_words = []
+        for a, longest in enumerate((LAST * C, WORD1_CUTS[1])):
+            words = place(2, [P, window_width(longest)], U32, 4, "token_words%d" % a)
             nc.vector.memset(words[:, T:].bitcast(I32), 0)
-            words_all.append(words)
+            token_words.append(words)
 
         raw = {}
-        x_view = xT.rearrange("(a p j) t -> a p j t", p=P, j=4)
+        x_view = xT.rearrange("(a p j) t -> a p j t", p=P, j=PACK)
         for a in range(PASSES):
-            for lo, hi in zip(LOADS[a], LOADS[a][1:]):
-                chunk = place(0, [P, 4, hi - lo], F32, 4, "raw%d_%d" % (a, lo))
-                nc.sync.dma_start(out=chunk[:], in_=x_view[a, :, :, lo:hi])
-                raw[a, lo] = chunk
+            for lo, hi in pieces(X_CUTS[a]):
+                raw[a, lo] = place(0, [P, PACK, hi - lo], F32, 4, "raw%d_%d" % (a, lo))
+                nc.sync.dma_start(out=raw[a, lo][:], in_=x_view[a, :, :, lo:hi])
             if a == 0:
                 nc.sync.dma_start(out=offs_sb[:], in_=offs)
         s_view = w_scales.rearrange("e a q n -> q (e a) n")
-        for q in range(4):
-            nc.sync.dma_start(out=ws[32 * q : 32 * q + 4, :, :].bitcast(I32), in_=s_view[4 * q : 4 * q + 4, :, :].bitcast(I32))
-        ww = place(4, [P, PASSES, E, 4 * N], U8, 1, "ww")
+        for g in range(4):
+            nc.sync.dma_start(out=w_bytes[32 * g : 32 * g + 4, :, :].bitcast(I32), in_=s_view[4 * g : 4 * g + 4, :, :].bitcast(I32))
+        w_codes = place(4, [P, PASSES, E, PACK * N], U8, 1, "w_codes")
         w_view = w_words.rearrange("e a p n r -> a p e (n r)")
-        for a, lo, hi in W_LOADS:
-            nc.sync.dma_start(out=ww[:, a, lo:hi, :], in_=w_view[a, :, lo:hi, :])
-        nc.sync.dma_start(out=ww[:, :, E - 1, :], in_=w_words[E - 1].rearrange("a p n r -> p a (n r)"))
+        for a in range(PASSES):
+            for lo, hi in pieces(W_CUTS):
+                nc.sync.dma_start(out=w_codes[:, a, lo:hi, :], in_=w_view[a, :, lo:hi, :])
+        nc.sync.dma_start(out=w_codes[:, :, LAST, :], in_=w_words[LAST].rearrange("a p n r -> p a (n r)"))
         gates = place(6, [P, 2, T], F32, 4, "gates")
         nc.sync.dma_start(out=pos1_sb[:], in_=pos1)
         nc.sync.dma_start(out=gates[:, 0, :], in_=gate[0])
         nc.sync.dma_start(out=pos2_sb[:], in_=pos2)
         nc.sync.dma_start(out=gates[:, 1, :], in_=gate[1])
 
-        words_slot = place(3, [P, PASSES, SLOTS], U32, 4, "words_slot")
-        bytes_slot = place(3, [P, SLOTS], U8, 1, "bytes_slot")
-
-        def gather(dst, window, idx, lo, hi):
-            nc.vector.tensor_copy(out=dst, in_=window[:, : max(T, (hi - lo) * 11 // 8)].indirect(idx[:, lo // 16 : hi // 16]))
-
-        grouped = {(a, lo): place(1, [P, HALF, 4], BF16, 2, "grouped%d_%d" % (a, lo)) for a in range(PASSES) for lo in (0, HALF)}
+        slot_words = place(3, [P, PASSES, SLOTS], U32, 4, "slot_words")
+        slot_bytes = place(3, [P, SLOTS], U8, 1, "slot_bytes")
+        grouped = {(a, lo): place(1, [P, HALF, PACK], BF16, 2, "grouped%d_%d" % (a, lo)) for a in range(PASSES) for lo in (0, HALF)}
 
         def rows(a, lo, hi):
             start = lo // HALF * HALF
             return grouped[a, start][:, lo - start : hi - start, :]
 
         def interleave(copy, a, lo, hi):
-            start = max(cut for cut in LOADS[a] if cut <= lo)
+            start = max(cut for cut in X_CUTS[a] if cut <= lo)
             dst = rows(a, lo, hi).rearrange("p (b i) j -> p b j i", i=4)
             src = raw[a, start][:, :, lo - start : hi - start].rearrange("p j (b i) -> p b j i", i=4)
             copy(out=dst, in_=src)
 
         def quantise(a, lo, hi):
             nc.vector.quantize_mx(
-                out=words_all[a][:, lo:hi].bitcast(FP8X4),
-                scales=bytes_all[4 * a :, lo:hi],
+                out=token_words[a][:, lo:hi].bitcast(FP8X4),
+                scales=token_bytes[4 * a :, lo:hi],
                 in_=rows(a, lo, hi).rearrange("p t j -> p (t j)"),
             )
 
-        interleave(nc.scalar.copy, 0, 160, 256)
-        interleave(nc.vector.tensor_copy, 0, 0, 160)
-        quantise(0, 0, 256)
-        interleave(nc.scalar.copy, 0, 320, 384)
-        interleave(nc.vector.tensor_copy, 0, 256, 320)
-        interleave(nc.scalar.copy, 0, 448, 512)
-        interleave(nc.vector.tensor_copy, 0, 384, 448)
-        quantise(0, 256, 384)
-        quantise(0, 384, 512)
-        gather(words_slot[:, 0, : SLOTS - C], words_all[0], offs_sb, 0, SLOTS - C)
-        for lo, hi in zip(LOADS[1], LOADS[1][1:]):
+        def gather(dst, window, lo, hi):
+            nc.vector.tensor_copy(out=dst, in_=window[:, : window_width(hi - lo)].indirect(entries(offs_sb, lo, hi)))
+
+        for (lo, hi), share in zip(pieces(X_CUTS[0]), VECTOR_SHARES):
+            interleave(nc.scalar.copy, 0, lo + share, hi)
+            interleave(nc.vector.tensor_copy, 0, lo, lo + share)
+            if lo == 0:
+                quantise(0, lo, hi)
+        for lo, hi in pieces(QUANT_CUTS)[1:]:
+            quantise(0, lo, hi)
+        gather(slot_words[:, 0, : LAST * C], token_words[0], 0, LAST * C)
+
+        for lo, hi in pieces(X_CUTS[1]):
             interleave(nc.scalar.copy, 1, lo, hi)
-        quantise(1, 0, 256)
-        quantise(1, 256, 384)
-        quantise(1, 384, 512)
-        words_last = keep.tile([P, C], U32, name="words_last", align_bytes=256, offset=(2 * T - 128) * 16)
-        gather(words_last[:], words_all[0], offs_sb, SLOTS - C, SLOTS)
+        for lo, hi in pieces(QUANT_CUTS):
+            quantise(1, lo, hi)
+        last_load = (PASSES * T - (T - X_CUTS[1][-2])) * PACK * 4
+        last_words = keep.tile([P, C], U32, name="last_words", align_bytes=ALIGN, offset=last_load)
+        gather(last_words[:], token_words[0], LAST * C, SLOTS)
 
         y = place(5, [P, SLOTS], F32, 4, "y")
         sums = [psum.tile([N, (hi - lo) * C], F32, name="sums%d" % lo) for lo, hi in BANKS]
 
         def multiply(e, a):
-            b = max(i for i, (lo, hi) in enumerate(BANKS) if lo <= e)
-            lo, hi = BANKS[b]
+            bank = max(i for i, (lo, hi) in enumerate(BANKS) if lo <= e)
+            lo, hi = BANKS[bank]
             cols = slice(e * C, (e + 1) * C)
             nc.tensor.matmul_mx(
-                out=sums[b][:, (e - lo) * C : (e - lo + 1) * C],
-                lhsT=ww[:, a, e, :].bitcast(FP8X4),
-                lhsT_scale=ws[:, e * PASSES + a, :],
-                rhs=(words_last[:] if (e, a) == (E - 1, 0) else words_slot[:, a, cols]).bitcast(FP8X4),
-                rhs_scale=bytes_slot[4 * a :, cols],
+                out=sums[bank][:, (e - lo) * C : (e - lo + 1) * C],
+                lhsT=w_codes[:, a, e, :].bitcast(FP8X4),
+                lhsT_scale=w_bytes[:, e * PASSES + a, :],
+                rhs=(last_words[:] if (e, a) == (LAST, 0) else slot_words[:, a, cols]).bitcast(FP8X4),
+                rhs_scale=slot_bytes[4 * a :, cols],
                 start=(a == 0 and e == lo),
                 stop=(a == PASSES - 1 and e == hi - 1),
             )
 
-        byte_ends = dict(zip(BYTE_CUTS, BYTE_CUTS[1:]))
-        for lo, hi in zip(WORD1_CUTS, WORD1_CUTS[1:]):
+        byte_ends = dict(pieces(BYTE_CUTS))
+        for lo, hi in pieces(WORD1_CUTS):
             if lo in byte_ends:
-                gather(bytes_slot[:, lo : byte_ends[lo]], bytes_all, offs_sb, lo, byte_ends[lo])
+                gather(slot_bytes[:, lo : byte_ends[lo]], token_bytes, lo, byte_ends[lo])
                 for e in range(lo // C, byte_ends[lo] // C):
                     multiply(e, 0)
-            gather(words_slot[:, 1, lo:hi], words_all[1], offs_sb, lo, hi)
+            gather(slot_words[:, 1, lo:hi], token_words[1], lo, hi)
             for e in range(lo // C, hi // C):
                 multiply(e, 1)
-        for b, (lo, hi) in enumerate(BANKS):
-            nc.scalar.copy(out=y[:, lo * C : hi * C], in_=sums[b][:])
+        for bank, (lo, hi) in enumerate(BANKS):
+            nc.scalar.copy(out=y[:, lo * C : hi * C], in_=sums[bank][:])
 
         first = place(1, [N, T], F32, 4, "first")
         fetched = place(3, [N, T], F32, 4, "fetched")
         second = place(2, [N, T], F32, 4, "second")
-        halves = list(zip(SECOND_CUTS, SECOND_CUTS[1:]))
-        for lo, hi in halves:
-            nc.scalar.activation(fetched[:, lo:hi], y[:].indirect(pos2_sb[:, lo // 16 : hi // 16]), COPY)
+        for lo, hi in pieces(SECOND_CUTS):
+            nc.scalar.activation(fetched[:, lo:hi], y[:].indirect(entries(pos2_sb, lo, hi)), COPY)
         nc.vector.tensor_tensor(first[:], y[:].indirect(pos1_sb[:]), gates[:, 0, :], MULT)
-        for lo, hi in halves:
+        for lo, hi in pieces(SECOND_CUTS):
             nc.vector.tensor_tensor(second[:, lo:hi], fetched[:, lo:hi], gates[:, 1, lo:hi], MULT)
-        for lo, hi in zip(OUT_CUTS, OUT_CUTS[1:]):
+        for lo, hi in pieces(OUT_CUTS):
             total = place(0, [N, hi - lo], F32, 4, "total%d" % lo)
             nc.vector.tensor_tensor(total[:], first[:, lo:hi], second[:, lo:hi], ADD)
             nc.sync.dma_start(out=out[:, lo:hi], in_=total[:])

@@ -29,7 +29,7 @@ QUANT_CUTS = (0, 256, 384, 512)
 BYTE_CUTS = (0, LAST * C, SLOTS)
 WORD1_CUTS = (0, 4 * C, LAST * C, SLOTS)
 BANKS = ((0, 2), (2, 4), (4, 5), (5, 6), (6, 7), (7, 8))
-W_CUTS = (0, 4, LAST)
+W_CUTS = ((0, 4, LAST), (0, 2, 4, LAST))
 SECOND_CUTS = (0, 320, T)
 OUT_CUTS = (0, 256, 384, T)
 REGION = 32768
@@ -87,17 +87,16 @@ def tile_routed_moe_kernel(tc, xT, w_words, w_scales, gate, offs, pos1, pos2, ou
         s_view = w_scales.rearrange("e a q n -> q (e a) n")
         for g in range(4):
             nc.sync.dma_start(out=w_bytes[32 * g : 32 * g + 4, :, :].bitcast(I32), in_=s_view[4 * g : 4 * g + 4, :, :].bitcast(I32))
+        nc.sync.dma_start(out=pos1_sb[:], in_=pos1)
         w_codes = place(4, [P, PASSES, E, PACK * N], U8, 1, "w_codes")
         w_view = w_words.rearrange("e a p n r -> a p e (n r)")
         for a in range(PASSES):
-            for lo, hi in pieces(W_CUTS):
+            for lo, hi in pieces(W_CUTS[a]):
                 nc.sync.dma_start(out=w_codes[:, a, lo:hi, :], in_=w_view[a, :, lo:hi, :])
         nc.sync.dma_start(out=w_codes[:, :, LAST, :], in_=w_words[LAST].rearrange("a p n r -> p a (n r)"))
         gates = place(6, [P, 2, T], F32, 4, "gates")
-        nc.sync.dma_start(out=pos1_sb[:], in_=pos1)
-        nc.sync.dma_start(out=gates[:, 0, :], in_=gate[0])
         nc.sync.dma_start(out=pos2_sb[:], in_=pos2)
-        nc.sync.dma_start(out=gates[:, 1, :], in_=gate[1])
+        nc.sync.dma_start(out=gates[:], in_=gate.rearrange("r n t -> n r t"))
 
         slot_words = place(3, [P, PASSES, SLOTS], U32, 4, "slot_words")
         slot_bytes = place(3, [P, SLOTS], U8, 1, "slot_bytes")

@@ -31,7 +31,7 @@ WORD1_CUTS = (0, 4 * C, LAST * C, SLOTS)
 BANKS = ((0, 2), (2, 4), (4, 5), (5, 6), (6, 7), (7, 8))
 W_CUTS = ((0, 4, LAST), (0, 2, 4, LAST))
 SECOND_CUTS = (0, 320, T)
-OUT_CUTS = (0, 256, 384, T)
+OUT_CUTS = (0, 128, 320, T)
 REGION = 32768
 ALIGN = 256
 HALF = T // 2
@@ -108,8 +108,8 @@ def tile_routed_moe_kernel(tc, xT, w_words, w_scales, gate, offs, pos1, pos2, ou
 
         def interleave(copy, a, lo, hi):
             start = max(cut for cut in X_CUTS[a] if cut <= lo)
-            dst = rows(a, lo, hi).rearrange("p (b i) j -> p b j i", i=4)
-            src = raw[a, start][:, :, lo - start : hi - start].rearrange("p j (b i) -> p b j i", i=4)
+            dst = rows(a, lo, hi).rearrange("p (b i) j -> p b j i", i=2)
+            src = raw[a, start][:, :, lo - start : hi - start].rearrange("p j (b i) -> p b j i", i=2)
             copy(out=dst, in_=src)
 
         def quantise(a, lo, hi):

@@ -98,8 +98,8 @@ def tile_routed_moe_kernel(tc, xT, w_words, w_scales, gate, offs, pos1, pos2, ou
         nc.sync.dma_start(out=pos2_sb[:], in_=pos2)
         nc.sync.dma_start(out=gates[:], in_=gate.rearrange("r n t -> n r t"))
 
-        slot_words = place(3, [P, PASSES, SLOTS], U32, 4, "slot_words")
-        slot_bytes = place(3, [P, SLOTS], U8, 1, "slot_bytes")
+        slot_words = place(5, [P, PASSES, SLOTS], U32, 4, "slot_words")
+        slot_bytes = place(5, [P, SLOTS], U8, 1, "slot_bytes")
         grouped = {(a, lo): place(1, [P, HALF, PACK], BF16, 2, "grouped%d_%d" % (a, lo)) for a in range(PASSES) for lo in (0, HALF)}
 
         def rows(a, lo, hi):
@@ -139,7 +139,7 @@ def tile_routed_moe_kernel(tc, xT, w_words, w_scales, gate, offs, pos1, pos2, ou
         last_words = keep.tile([P, C], U32, name="last_words", align_bytes=ALIGN, offset=last_load)
         gather(last_words[:], token_words[0], LAST * C, SLOTS)
 
-        y = place(5, [P, SLOTS], F32, 4, "y")
+        y = place(3, [P, SLOTS], F32, 4, "y")
         sums = [psum.tile([N, (hi - lo) * C], F32, name="sums%d" % lo) for lo, hi in BANKS]
 
         def multiply(e, a):
@@ -168,9 +168,9 @@ def tile_routed_moe_kernel(tc, xT, w_words, w_scales, gate, offs, pos1, pos2, ou
         for bank, (lo, hi) in enumerate(BANKS):
             nc.scalar.copy(out=y[:, lo * C : hi * C], in_=sums[bank][:])
 
-        first = place(1, [N, T], F32, 4, "first")
-        fetched = place(3, [N, T], F32, 4, "fetched")
-        second = place(2, [N, T], F32, 4, "second")
+        first = place(6, [N, T], F32, 4, "first")
+        fetched = place(6, [N, T], F32, 4, "fetched")
+        second = place(6, [N, T], F32, 4, "second")
         for lo, hi in pieces(SECOND_CUTS):
             nc.scalar.activation(fetched[:, lo:hi], y[:].indirect(entries(pos2_sb, lo, hi)), COPY)
         nc.vector.tensor_tensor(first[:], y[:].indirect(pos1_sb[:]), gates[:, 0, :], MULT)

@@ -30,8 +30,7 @@ BYTE_CUTS = (0, LAST * C, SLOTS)
 WORD1_CUTS = (0, 4 * C, LAST * C, SLOTS)
 BANKS = ((0, 2), (2, 4), (4, 5), (5, 6), (6, 7), (7, 8))
 W_CUTS = ((0, 4, LAST), (0, 2, 4, LAST))
-SECOND_CUTS = (0, 320, T)
-OUT_CUTS = (0, 128, 320, T)
+OUT_CUTS = (0, 128, 384, T)
 REGION = 32768
 ALIGN = 256
 HALF = T // 2
@@ -171,12 +170,18 @@ def tile_routed_moe_kernel(tc, xT, w_words, w_scales, gate, offs, pos1, pos2, ou
         first = place(6, [N, T], F32, 4, "first")
         fetched = place(6, [N, T], F32, 4, "fetched")
         second = place(6, [N, T], F32, 4, "second")
-        for lo, hi in pieces(SECOND_CUTS):
+        cuts = pieces(OUT_CUTS)
+        for lo, hi in cuts:
             nc.scalar.activation(fetched[:, lo:hi], y[:].indirect(entries(pos2_sb, lo, hi)), COPY)
         nc.vector.tensor_tensor(first[:], y[:].indirect(pos1_sb[:]), gates[:, 0, :], MULT)
-        for lo, hi in pieces(SECOND_CUTS):
+
+        def weigh(lo, hi):
             nc.vector.tensor_tensor(second[:, lo:hi], fetched[:, lo:hi], gates[:, 1, lo:hi], MULT)
-        for lo, hi in pieces(OUT_CUTS):
+
+        weigh(*cuts[0])
+        for i, (lo, hi) in enumerate(cuts):
+            if i + 1 < len(cuts):
+                weigh(*cuts[i + 1])
             total = place(0, [N, hi - lo], F32, 4, "total%d" % lo)
             nc.vector.tensor_tensor(total[:], first[:, lo:hi], second[:, lo:hi], ADD)
             nc.sync.dma_start(out=out[:, lo:hi], in_=total[:])

import math
from contextlib import ExitStack

import concourse.mybir as mybir

K, T, E, C, N = 1024, 512, 8, 128, 128
SLOTS = E * C
PASSES = K // 512
P = 128
PACK = 4
PER_COLUMN = 16
LAST = E - 1
FLOPS = 2 * K * SLOTS * N

F32 = mybir.dt.float32
BF16 = mybir.dt.bfloat16
U32 = mybir.dt.uint32
I32 = mybir.dt.int32
U16 = mybir.dt.uint16
U8 = mybir.dt.uint8
FP8X4 = mybir.dt.float8_e4m3fn_x4
MULT = mybir.AluOpType.mult
ADD = mybir.AluOpType.add
COPY = mybir.ActivationFunctionType.Copy

X_CUTS = ((0, 256, 384, 512), (0, 128, 256, 384, 512))
VECTOR_SHARES = (160, 64, 64)
QUANT_CUTS = (0, 256, 384, 512)
BYTE_CUTS = (0, LAST * C, SLOTS)
WORD1_CUTS = (0, 4 * C, LAST * C, SLOTS)
BANKS = ((0, 2), (2, 4), (4, 5), (5, 6), (6, 7), (7, 8))
W_CUTS = ((0, 4, LAST), (0, 2, 4, LAST))
OUT_CUTS = (0, 128, 384, T)
REGION = 32768
ALIGN = 256
HALF = T // 2


def pieces(cuts):
    return list(zip(cuts, cuts[1:]))


def window_width(entries):
    return max(T, entries * 11 // 8)


def tile_routed_moe_kernel(tc, xT, w_words, w_scales, gate, offs, pos1, pos2, out):
    nc = tc.nc
    with ExitStack() as ctx:
        lists = ctx.enter_context(tc.tile_pool(name="lists", bufs=1))
        keep = ctx.enter_context(tc.tile_pool(name="keep", bufs=1))
        psum = ctx.enter_context(tc.psum_pool(name="psum", bufs=1))

        offs_sb = lists.tile([P, SLOTS // PER_COLUMN], U16, name="offs_sb")
        pos1_sb = lists.tile([P, T // PER_COLUMN], U16, name="pos1_sb")
        pos2_sb = lists.tile([P, T // PER_COLUMN], U16, name="pos2_sb")

        free = {}

        def place(region, shape, dtype, itemsize, name):
            start = free.get(region, region * REGION)
            free[region] = start + (itemsize * math.prod(shape[1:]) + ALIGN - 1) // ALIGN * ALIGN
            return keep.tile(shape, dtype, name=name, align_bytes=ALIGN, offset=start)

        def entries(list_tile, lo, hi):
            return list_tile[:, lo // PER_COLUMN : hi // PER_COLUMN]

        w_bytes = place(4, [P, E * PASSES, N], U8, 1, "w_bytes")
        nc.gpsimd.memset(w_bytes[:].rearrange("p b n -> p (b n)").bitcast(I32), 0)
        token_bytes = place(2, [P, window_width(BYTE_CUTS[1])], U8, 1, "token_bytes")
        nc.gpsimd.memset(token_bytes[:].bitcast(I32), 0)
        token_words = []
        for a, longest in enumerate((LAST * C, WORD1_CUTS[1])):
            words = place(2, [P, window_width(longest)], U32, 4, "token_words%d" % a)
            nc.vector.memset(words[:, T:].bitcast(I32), 0)
            token_words.append(words)

        raw = {}
        x_view = xT.rearrange("(a p j) t -> a p j t", p=P, j=PACK)
        for a in range(PASSES):
            for lo, hi in pieces(X_CUTS[a]):
                raw[a, lo] = place(0, [P, PACK, hi - lo], F32, 4, "raw%d_%d" % (a, lo))
                nc.sync.dma_start(out=raw[a, lo][:], in_=x_view[a, :, :, lo:hi])
            if a == 0:
                nc.sync.dma_start(out=offs_sb[:], in_=offs)
        s_view = w_scales.rearrange("e a q n -> q (e a) n")
        for g in range(4):
            nc.sync.dma_start(out=w_bytes[32 * g : 32 * g + 4, :, :].bitcast(I32), in_=s_view[4 * g : 4 * g + 4, :, :].bitcast(I32))
        nc.sync.dma_start(out=pos1_sb[:], in_=pos1)
        w_codes = place(4, [P, PASSES, E, PACK * N], U8, 1, "w_codes")
        w_view = w_words.rearrange("e a p n r -> a p e (n r)")
        for a in range(PASSES):
            for lo, hi in pieces(W_CUTS[a]):
                nc.sync.dma_start(out=w_codes[:, a, lo:hi, :], in_=w_view[a, :, lo:hi, :])
        nc.sync.dma_start(out=w_codes[:, :, LAST, :], in_=w_words[LAST].rearrange("a p n r -> p a (n r)"))
        gates = place(6, [P, 2, T], F32, 4, "gates")
        nc.sync.dma_start(out=pos2_sb[:], in_=pos2)
        nc.sync.dma_start(out=gates[:], in_=gate.rearrange("r n t -> n r t"))

        slot_words = place(5, [P, PASSES, SLOTS], U32, 4, "slot_words")
        slot_bytes = place(5, [P, SLOTS], U8, 1, "slot_bytes")
        grouped = {(a, lo): place(1, [P, HALF, PACK], BF16, 2, "grouped%d_%d" % (a, lo)) for a in range(PASSES) for lo in (0, HALF)}

        def rows(a, lo, hi):
            start = lo // HALF * HALF
            return grouped[a, start][:, lo - start : hi - start, :]

        def interleave(copy, a, lo, hi):
            start = max(cut for cut in X_CUTS[a] if cut <= lo)
            dst = rows(a, lo, hi).rearrange("p (b i) j -> p b j i", i=2)
            src = raw[a, start][:, :, lo - start : hi - start].rearrange("p j (b i) -> p b j i", i=2)
            copy(out=dst, in_=src)

        def quantise(a, lo, hi):
            nc.vector.quantize_mx(
                out=token_words[a][:, lo:hi].bitcast(FP8X4),
                scales=token_bytes[4 * a :, lo:hi],
                in_=rows(a, lo, hi).rearrange("p t j -> p (t j)"),
            )

        def gather(dst, window, lo, hi):
            nc.vector.tensor_copy(out=dst, in_=window[:, : window_width(hi - lo)].indirect(entries(offs_sb, lo, hi)))

        for (lo, hi), share in zip(pieces(X_CUTS[0]), VECTOR_SHARES):
            interleave(nc.scalar.copy, 0, lo + share, hi)
            interleave(nc.vector.tensor_copy, 0, lo, lo + share)
            if lo == 0:
                quantise(0, lo, hi)
        for lo, hi in pieces(QUANT_CUTS)[1:]:
            quantise(0, lo, hi)
        gather(slot_words[:, 0, : LAST * C], token_words[0], 0, LAST * C)

        for lo, hi in pieces(X_CUTS[1]):
            interleave(nc.scalar.copy, 1, lo, hi)
        for lo, hi in pieces(QUANT_CUTS):
            quantise(1, lo, hi)
        last_load = (PASSES * T - (T - X_CUTS[1][-2])) * PACK * 4
        last_words = keep.tile([P, C], U32, name="last_words", align_bytes=ALIGN, offset=last_load)
        gather(last_words[:], token_words[0], LAST * C, SLOTS)

        y = place(3, [P, SLOTS], F32, 4, "y")
        sums = [psum.tile([N, (hi - lo) * C], F32, name="sums%d" % lo) for lo, hi in BANKS]

        def multiply(e, a):
            bank = max(i for i, (lo, hi) in enumerate(BANKS) if lo <= e)
            lo, hi = BANKS[bank]
            cols = slice(e * C, (e + 1) * C)
            nc.tensor.matmul_mx(
                out=sums[bank][:, (e - lo) * C : (e - lo + 1) * C],
                lhsT=w_codes[:, a, e, :].bitcast(FP8X4),
                lhsT_scale=w_bytes[:, e * PASSES + a, :],
                rhs=(last_words[:] if (e, a) == (LAST, 0) else slot_words[:, a, cols]).bitcast(FP8X4),
                rhs_scale=slot_bytes[4 * a :, cols],
                start=(a == 0 and e == lo),
                stop=(a == PASSES - 1 and e == hi - 1),
            )

        byte_ends = dict(pieces(BYTE_CUTS))
        for lo, hi in pieces(WORD1_CUTS):
            if lo in byte_ends:
                gather(slot_bytes[:, lo : byte_ends[lo]], token_bytes, lo, byte_ends[lo])
                for e in range(lo // C, byte_ends[lo] // C):
                    multiply(e, 0)
            gather(slot_words[:, 1, lo:hi], token_words[1], lo, hi)
            for e in range(lo // C, hi // C):
                multiply(e, 1)
        for bank, (lo, hi) in enumerate(BANKS):
            nc.scalar.copy(out=y[:, lo * C : hi * C], in_=sums[bank][:])

        first = place(6, [N, T], F32, 4, "first")
        fetched = place(6, [N, T], F32, 4, "fetched")
        second = place(6, [N, T], F32, 4, "second")
        cuts = pieces(OUT_CUTS)
        for lo, hi in cuts:
            nc.scalar.activation(fetched[:, lo:hi], y[:].indirect(entries(pos2_sb, lo, hi)), COPY)
        nc.vector.tensor_tensor(first[:], y[:].indirect(pos1_sb[:]), gates[:, 0, :], MULT)

        def weigh(lo, hi):
            nc.vector.tensor_tensor(second[:, lo:hi], fetched[:, lo:hi], gates[:, 1, lo:hi], MULT)

        weigh(*cuts[0])
        for i, (lo, hi) in enumerate(cuts):
            if i + 1 < len(cuts):
                weigh(*cuts[i + 1])
            total = place(0, [N, hi - lo], F32, 4, "total%d" % lo)
            nc.vector.tensor_tensor(total[:], first[:, lo:hi], second[:, lo:hi], ADD)
            nc.sync.dma_start(out=out[:, lo:hi], in_=total[:])
